import numpy as np, ml_dtypes
CORES = [40,64,80,88,96,104,120,144]
N = 8
BF = ml_dtypes.bfloat16
def gentries(a):
    return np.ascontiguousarray(a.reshape(8, 16, -1).transpose(0, 2, 1)).reshape(8, -1)
def gtable(e):
    e = np.asarray(e); return np.ascontiguousarray(e.reshape(8, -1, 16).transpose(0, 2, 1)).reshape(128, -1).astype(np.int32)
ND, NR, L, CAP, HB, LV, RO = 1024, 2048, 256, 32, 3, 4, 2
def parts(rng):
    cold = rng.random((N, 8, 1, NR)) < 0.4; cold[..., 5] = True
    regs = rng.integers(-15, 16, (N, 8, 16, NR)); warm = rng.random(regs.shape) < rng.random((N, 8, 1, NR))
    regs = np.where(cold | ~warm, -np.abs(regs), regs)
    acts = rng.integers(0, NR, (N, 8, 16, ND)); dead = rng.random((N, 8, 1, ND)) < 0.125
    order = np.argsort(~cold[:, :, 0], axis=-1, kind="stable"); cnt = np.add.reduce(cold[:, :, 0].astype(np.int64), axis=-1)
    pick = (rng.random(acts.shape) * cnt[:, :, None, None]).astype(np.int64).reshape(N, 8, -1)
    acts = np.where(dead, np.take_along_axis(order, pick, 2).reshape(acts.shape), acts)
    return acts, regs, rng.integers(0, 16, (N, 8, 16, ND)), rng.integers(0, ND, (N, 8, L)), rng.integers(1, 16, (N, 8, 16, L)), rng.integers(0, 64, (N, 8, RO, LV, L))
def pack(acts, regs, pay, n0, rch, dr):
    b = lambda a: np.ascontiguousarray(a.reshape(N, 128, -1)).astype(np.float32).astype(BF)
    return {"acts": np.ascontiguousarray(acts.reshape(N, 128, ND)).astype(np.int32), "regs": b(regs), "pay": b(pay), "n0": np.stack([gtable(a) for a in n0]), "rch": b(rch),
            "dr": np.ascontiguousarray(dr.reshape(N, 8, RO * LV * L)).astype(np.int32)}
def setup_inputs(rng):
    return pack(*parts(rng))
def setup_inputs_room(rng):
    acts, regs, pay, n0, rch, dr = parts(rng)
    regs[:, ::2] = -rng.integers(2 * RO, 16, (N, 4, 16, NR)); pay = pay * rng.integers(0, 2, pay.shape)
    for q in range(N):
        for g in range(0, 8, 2):
            for t in range(RO):
                p = int(rng.integers(0, 4))
                if q == 0: p = (g // 2 + (t if g else 0)) % 4
                c = np.zeros(N, np.int64)
                if p == 0: c[:] = CAP
                elif p == 1: c[::2] = CAP + 1; c[1::2] = CAP - 1
                elif p == 2: c[0] = L
                else: c[1] = 1; c[2] = CAP; c[3] = L - 1 - CAP
                to = rng.permutation(np.repeat(np.arange(N), np.roll(c, int(rng.integers(0, N)))))
                dr[q, g, t, HB - 1] = to + N * rng.integers(0, 64 // N, L)
    return pack(acts, regs, pay, n0, rch, dr)
def setup_inputs_ties(rng):
    acts, regs, pay, n0, rch, dr = parts(rng)
    for g in (0, 3, 6):
        regs[:, g] = 15; rch[:, g] = rng.integers(1, 16 - 2 * RO, (N, 16, L))
        dr[:, g] = rng.choice(np.concatenate([4 * np.arange(16), 4 * np.arange(1, 16) - 1, np.array([63])]), (N, RO, LV, L))
    for g in (1, 4):
        i = rng.integers(0, 16, (N, 1, NR)); one = (np.arange(16)[None, :, None] == i) & (rng.random((N, 1, NR)) < 0.25)
        regs[:, g] = np.where(one, 1, -rng.integers(0, 16, (N, 16, NR)))
        dr[:, g] = 8 * rng.integers(0, 8, (N, RO, LV, L))
    for g in (2, 5, 7):
        dr[:, g] = rng.choice(np.array([0, 1, 31, 32, 62, 63]), (N, RO, LV, L))
    return pack(acts, regs, pay, n0, rch, dr)
def setup_inputs_alike(rng):
    acts, regs, pay, n0, rch, dr = parts(rng)
    n0[:, ::2] = rng.choice(np.array([0, ND - 1, ND // 2, 3]), (N, 4, L))
    acts[:, 1] = rng.choice(np.array([0, NR - 1, 7, NR // 2]), (N, 16, ND))
    acts[:, 5] = rng.integers(NR - 64, NR, (N, 16, ND)); acts[:, 7] = rng.integers(0, 100, (N, 16, ND))
    acts[:, 2] = acts[:, 2, :1]
    dr[:, 4:] = dr[:, 4:, :, :, :1]
    return pack(acts, regs, pay, n0, rch, dr)
def setup_inputs_clip(rng):
    acts, regs, pay, n0, rch, dr = parts(rng)
    regs = rng.choice(np.array([-15, -14, -1, 0, 1, 14, 15]), (N, 8, 16, NR)); pay = 15 * rng.integers(0, 2, pay.shape)
    rch = np.where(rng.random(rch.shape) < 0.7, 15, rng.integers(1, 3, rch.shape))
    a, b = rng.permutation(8)[:2]
    regs[:, a] = 15; rch[:, a] = 15; regs[:, b] = -15
    return pack(acts, regs, pay, n0, rch, dr)
def setup_inputs_spread(rng):
    acts, regs, pay, n0, rch, dr = parts(rng)
    u = lambda shape: np.minimum((np.exp2(4 * rng.random((N, 8, 1, shape[-1]))) * rng.random(shape)).astype(np.int64), 15)
    regs = u(regs.shape) * np.where(rng.random(regs.shape) < rng.random((N, 8, 1, NR)), 1, -1)
    pay = u(pay.shape); rch = np.maximum(u(rch.shape), 1)
    dr = np.minimum((64 * rng.random(dr.shape) ** np.exp2(4 * rng.random((N, 8, 1, 1, L)) - 2)).astype(np.int64), 63)
    return pack(acts, regs, pay, n0, rch, dr)
def check_inputs(d):
    bad = []
    for k, lo, hi in (("acts", 0, NR - 1), ("regs", -15, 15), ("pay", 0, 15), ("n0", 0, ND - 1), ("rch", 1, 15), ("dr", 0, 63)):
        a = np.asarray(d[k]).astype(np.float64)
        if not (np.min(a) >= lo and np.max(a) <= hi): bad.append("range of " + k)
        elif not np.all(a == np.rint(a)): bad.append("whole numbers in " + k)
    return bad
def level(rg, ac, n, x, v, e):
    S = n.shape[1]
    a = np.take_along_axis(ac, n[:, None, :], 2)
    p = np.maximum(np.take_along_axis(rg, a.reshape(8, 1, 16 * S), 2), 0).reshape(8, 16, 16, S)
    c = np.add.accumulate(np.add.reduce(np.minimum(x[:, :, None, :], p), axis=1), axis=1)
    tot = c[:, 15]
    k = np.where(tot > 0, np.argmax(64 * c > (v * tot)[:, None, :], axis=1), v & 15)
    rec = np.take_along_axis(a, k[:, None, :], 1)[:, 0]
    x = np.minimum(x, np.take_along_axis(p, k[:, None, None, :], 2)[:, :, 0] + 1)
    return k, rec, x, (5 * rec + 13 * n + e) & (ND - 1)
def rewrite(rg, rec, live, w):
    for g in range(8):
        s = np.nonzero(live[g])[0]
        u, j = np.unique(rec[g, s], return_index=True)
        rg[g][:, u] = np.clip(rg[g][:, u] + w[g][:, s[j]], -15, 15)
def reference(acts, regs, pay, n0, rch, dr):
    ac = acts.astype(np.int64).reshape(N, 8, 16, ND); rg = regs.astype(np.float32).astype(np.int64).reshape(N, 8, 16, NR)
    py = pay.astype(np.float32).astype(np.int64).reshape(N, 8, 16, ND); x0 = rch.astype(np.float32).astype(np.int64).reshape(N, 8, 16, L)
    st = np.stack([gentries(a) for a in n0]).astype(np.int64); v = dr.astype(np.int64).reshape(N, 8, RO, LV, L)
    for t in range(RO):
        fn = np.zeros((N, 8, N * CAP), np.int64); fx = np.ones((N, 8, 16, N * CAP), np.int64); fv = np.zeros((N, 8, LV, N * CAP), np.int64); live = np.zeros((N, 8, N * CAP), bool)
        home = []
        for r in range(N):
            n, x, vt = st[r], x0[r], v[r, :, t]
            for e in range(1, HB + 1): k, rec, x, n = level(rg[r], ac[r], n, x, vt[:, e - 1], e)
            to = k & (N - 1); oh = (to[:, None, :] == np.arange(N)[None, :, None]).astype(np.int64)
            place = np.take_along_axis(np.add.accumulate(oh, axis=2), to[:, None, :], 1)[:, 0] - 1
            g, l = np.nonzero(place < CAP); d = to[g, l]; s = r * CAP + place[g, l]
            fn[d, g, s] = n[g, l]; fx[d, g, :, s] = x[g, :, l]; fv[d, g, :, s] = vt[g, :, l]; live[d, g, s] = True
            home.append((rec, g, l, d, s))
        recs, sg = [], []
        for q in range(N):
            n, x = fn[q], fx[q]
            for e in range(HB + 1, LV + 1): k, rec, x, n = level(rg[q], ac[q], n, x, fv[q, :, e - 1], e)
            val = np.minimum(np.take_along_axis(py[q], n[:, None, :], 2), x)
            recs.append(rec); sg.append(np.sign(16 * val - np.add.reduce(val, axis=1, keepdims=True)))
        for q in range(N): rewrite(rg[q], recs[q], live[q], sg[q])
        sg = np.stack(sg)
        for r in range(N):
            rec, g, l, d, s = home[r]
            w = np.zeros((8, 16, L), np.int64); went = np.zeros((8, L), bool)
            w[g, :, l] = -sg[d, g, :, s]; went[g, l] = True
            rewrite(rg[r], rec, went, w)
    return {"yr": rg.reshape(N, 128, NR).astype(np.float32).astype(BF)}

@@ -1,0 +1,688 @@
+from concourse.bass import DstId, RemoteDMATransfer
+from concourse.mybir import AluOpType as OP, AxisListType, ActivationFunctionType as AF
+
+BIG = float(1 << 22)
+F4, B2, I4, U2 = "float32", "bfloat16", "int32", "uint16"
+SCRATCH = {}
+for _d, _w, _s in (
+        (I4, 1024, "acs acn"), (F4, 1024, "da n13"), (B2, 2304, "rg"), (B2, 1024, "pys jk"), (B2, 256, "rc"), (I4, 16, "n0s"),
+        (I4, 128, "drp dr15"), (B2, 128, "drb drc one bm idn dz em qm gm"), (F4, 128, "bf1 bf5 b15 onf"), (B2, 2048, "lk ri bdx pt"),
+        (I4, 16, "pmi pma"), (I4, 256, "jj"), (F4, 8, "pc"), (F4, 16, "dg"), (F4, 256, "dd"), (B2, 2064, "cod"), (B2, 16, "cb"),
+        (F4, 16, "ta tb rw of pri0 pri1 ntr0 ntr1 dmp dv0 dv1 da0 da1"), (F4, 32, "tin tou recf ded"), (F4, 256, "posf0 posf1"),
+        (B2, 256, "pos0 pos1 xm0 xm xn xr b ff gg u4 val zb0 zb1 zg cl cr ch ci"), (F4, 1536, "vv"), (B2, 1536, "uu"), (F4, 512, "pk"),
+        (U2, 16, "n0u nu ru su zo rwu rwt"), (I4, 16, "nb0 ni nb t5 t6 yl ym"), (U2, 256, "a1 av"), (U2, 32, "ofu"), (B2, 4096, "r mn"),
+        (F4, 256, "thr mk mq sc ss cum y yx land0 land1 v4"), (I4, 256, "ti tj yi yj yk yo"), (F4, 2560, "win0 win1"),
+        (B2, 272, "zl0 zl1"), (F4, 64, "rl0 rl1"), (B2, 64, "rz0 rz1")):
+    for _n in _s.split():
+        SCRATCH[_n] = ("sbuf", [128, _w], _d)
+for _n in range(8):
+    SCRATCH["ps%d" % _n] = ("psum", [128, 512], F4)
+SEMAPHORES = ["sv", "ss", "sp", "sg", "loc"] + ["ld%d" % _i for _i in range(12)] + \
+    ["%s%d" % (_a, _t) for _a in ("ha", "hb", "za", "zb", "rq", "rv") for _t in range(2)]
+
+
+def bits(es):
+    m = 0
+    for e in es:
+        m |= 1 << e
+    return m
+
+
+def split(es, n):
+    w = len(es) // n
+    return [es[j * w:(j + 1) * w] for j in range(n)]
+
+
+def share(es, n):
+    out, left = [], list(es)
+    for j in range(n, 0, -1):
+        w = 1
+        while w * 2 * j <= len(left):
+            w *= 2
+        out.append(left[:w])
+        left = left[w:]
+    return out
+
+
+def places(core, T, topo):
+    same = [q for q in range(8) if T.cores[q] == core or topo.may_write(core, T.cores[q])]
+    return same, [q for q in range(8) if q not in same]
+
+
+def relays(core, T, topo):
+    other = places(core, T, topo)[1]
+    c = [d for d in topo.cores_of(core) if d != core and all(topo.may_write(d, T.cores[q]) for q in other)]
+    c.sort(key=lambda d: (topo.die(d) != topo.die(core), d))
+    return c[:2]
+
+
+def dst(d, src, topo):
+    rid, pid = topo.addr(d, src)
+    return DstId(rid=rid, pnc=pid)
+
+
+def helper(g, core, home, j, T, topo):
+    to = places(home, T, topo)[1][2 * j:2 * j + 2]
+    n = 0
+    off = topo.engines(core, T.cores[to[0]])
+    es = split([e for e in topo.engines(home, core) if e not in off], 2)[j]
+    for t in range(2):
+        for arr, buf, land, sem in (("rq", "rl", "land", "hb"), ("rv", "rz", "zl", "zb")):
+            g.wait_ge(T.sem["%s%d" % (arr, t)], len(es))
+            trs = []
+            for i, q in enumerate(to):
+                d = T.cores[q]
+                s2, o2 = places(d, T, topo)
+                p = (s2 + o2).index(T.rank_of(home))
+                ee = split(topo.engines(core, d), 2)[i]
+                trs.append(RemoteDMATransfer(dst_ids=[dst(d, core, topo)], dma_engine_mask=bits(ee), remote_sem=T.sem["%s%d" % (sem, t)],
+                                             src=T["%s%d" % (buf, t)][:, 32 * i:32 * i + 32], dst=T["%s%d" % (land, t)][:, 32 * p:32 * p + 32]))
+                n += len(ee)
+            g.remote_dma_fused(trs, local_sem=T.sem.loc)
+    g.wait_ge(T.sem.loc, n)
+
+
+def rank_program(g, core, T, topo):
+    me = T.rank_of(core)
+    if me is None:
+        for c in T.cores:
+            rel = relays(c, T, topo)
+            if core in rel:
+                helper(g, core, c, rel.index(core), T, topo)
+        return
+    same, other = places(core, T, topo)
+    order = same + other
+    pos = [order.index(q) for q in range(8)]
+    rel = relays(core, T, topo)
+
+    Q = {"V": g.vector, "S": g.scalar, "P": g.tensor, "G": g, "Y": g.sync}
+    SEM = {"V": "sv", "S": "ss", "P": "sp", "G": "sg"}
+    total, known, clocks = {}, {q: {} for q in Q}, {}
+    lastw, readers, bank = {}, {}, {}
+    nld, nloc = [0], [0]
+
+    def merge(a, b):
+        for k, v in b.items():
+            if a.get(k, 0) < v:
+                a[k] = v
+
+    def waits(q, unit, rd, wr, bk):
+        need = {}
+
+        def add(tok):
+            _, s, v = tok
+            if known[q].get(s, 0) < v and need.get(s, 0) < v:
+                need[s] = v
+        for k in rd:
+            if k in lastw:
+                add(lastw[k])
+        for k in wr:
+            if k in lastw and (lastw[k][0] != unit or unit != "P"):
+                add(lastw[k])
+            for u2, tok in readers.get(k, {}).items():
+                if u2 != unit:
+                    add(tok)
+        for k in bk:
+            for u2, tok in bank.get(k, {}).items():
+                if u2 != unit:
+                    add(tok)
+        items = list(need.items())
+        for s, v in items:
+            if not any(s2 != s and clocks[(s2, v2)].get(s, 0) >= v for s2, v2 in items):
+                Q[q].wait_ge(T.sem[s], v)
+        for s, v in items:
+            merge(known[q], clocks[(s, v)])
+
+    def note(q, unit, tok, rd, wr, bk):
+        c = dict(known[q])
+        merge(c, {tok[1]: tok[2]})
+        clocks[(tok[1], tok[2])] = c
+        for k in rd:
+            readers.setdefault(k, {})[unit] = tok
+        for k in wr:
+            lastw[k] = tok
+            readers[k] = {}
+        for k in bk:
+            bank.setdefault(k, {})[unit] = tok
+
+    def op(q, fn, rd, wr, bk=()):
+        waits(q, q, rd, wr, bk)
+        s = SEM[q]
+        total[s] = total.get(s, 0) + 1
+        fn(Q[q]).then_inc(T.sem[s], 1)
+        note(q, q, (q, s, total[s]), rd, wr, bk)
+
+    def dma(q, pairs, rd, wr):
+        s = "ld%d" % nld[0]
+        nld[0] += 1
+        waits(q, s, rd, wr, ())
+        for o, i in pairs:
+            Q[q].dma_start(o, i).then_inc(T.sem[s], 16)
+        total[s] = 16 * len(pairs)
+        note(q, s, (s, s, total[s]), rd, wr, ())
+
+    def ext(k, s, v):
+        total[s] = v
+        clocks[(s, v)] = {s: v}
+        lastw[k] = ("X", s, v)
+
+    def remote(trs, rd):
+        waits("G", "R", rd, (), ())
+        g.remote_dma_fused(trs, local_sem=T.sem.loc)
+
+    def tt(out, a, b_, o, rd, wr, bk=()):
+        op("V", lambda e: e.tensor_tensor(out, a, b_, o), rd, wr, bk)
+
+    def ts(out, a, s1, s2, o1, o2, rd, wr, bk=()):
+        if o2 is None:
+            op("V", lambda e: e.tensor_scalar(out, a, s1, None, o1), rd, wr, bk)
+        else:
+            op("V", lambda e: e.tensor_scalar(out, a, s1, s2, o1, o2), rd, wr, bk)
+
+    def cp(out, a, rd, wr, bk=()):
+        op("V", lambda e: e.tensor_copy(out, a), rd, wr, bk)
+
+    def ms(ap, c, wr):
+        op("V", lambda e: e.memset(ap, c), (), wr)
+
+    def act(out, a, f, rd, wr, bk=(), **kw):
+        op("S", lambda e: e.activation(out, a, f, **kw), rd, wr, bk)
+
+    def mm(out, l, r_, st, sp, rd, wr, bk):
+        op("P", lambda e: e.matmul(out, l, r_, st, sp), rd, wr, bk)
+
+    def sel(out, a, pat, o, fill, base, cm, rd, wr):
+        op("G", lambda e: e.affine_select(out, a, pat, o, fill, base, cm), rd, wr)
+
+    def iota(out, pat, base, cm, wr, flag=True):
+        if flag:
+            op("G", lambda e: e.iota(out, pat, base, cm, allow_small_or_imprecise_dtypes=True), (), wr)
+        else:
+            op("G", lambda e: e.iota(out, pat, base, cm), (), wr)
+
+    ps = [T["ps%d" % i] for i in range(8)]
+    XB = (4, 6)
+    H = lambda h: slice(128 * h, 128 * h + 128)
+    L8 = lambda h: slice(8 * h, 8 * h + 8)
+    BMP, BMQ = [[-16, 8], [0, 16]], [[16, 8], [0, 16]]
+
+    ms(T.one[:], 1.0, ["one"])
+    ms(T.acn[:], 0, ["acn"])
+    for n in ("em", "qm", "gm"):
+        ms(T[n][:], 0.0, [n])
+    dma("Y", [(T.n0s[:], T.n0[:])], (), ["n0s"])
+    dma("Y", [(T.acs[:], T.acts[:])], (), ["acs"])
+    dma("S", [(T.drp[:], T.dr[:])], (), ["drp"])
+    dma("S", [(T.rg[:, 0:2048], T.regs[:])], (), ["rg"])
+    dma("Y", [(T.rc[:], T.rch[:])], (), ["rc"])
+    dma("Y", [(T.acn[16 * q:16 * q + 15, :], T.acts[16 * q + 1:16 * q + 16, :]) for q in range(8)], (), ["acn"])
+    dma("Y", [(T.pys[:], T.pay[:])], (), ["pys"])
+
+    iota(T.pmi[:], [[0, 16]], 0, 1, ["pmi"], False)
+    sel(T.bm[:], T.one[:], BMP, OP.is_ge, 0.0, 0, 1, ["one"], ["bm"])
+    sel(T.bm[:], T.bm[:], BMQ, OP.is_ge, 0.0, 15, -1, ["bm"], ["bm"])
+    iota(T.jj[:], [[0, 16], [1, 16]], 0, 0, ["jj"], False)
+    sel(T.idn[:], T.one[:], [[-1, 128]], OP.is_equal, 0.0, 0, 1, ["one"], ["idn"])
+    ts(T.pma[:], T.pmi[:], 15, None, OP.bitwise_and, None, ["pmi"], ["pma"])
+    cp(T.pc[:, 0:1], T.pma[:, 0:1], ["pma"], ["pc0"])
+    ts(T.pc[:, 4:5], T.pc[:, 0:1], 1.0, 2.0 ** -17, OP.add, OP.mult, ["pc0"], ["pc4"])
+    ts(T.lk[:, 0:128], T.bm[:], 64.0, None, OP.mult, None, ["bm"], ["lk"])
+    ts(T.yx[:], T.jj[:], T.pc[:, 0:1], None, OP.subtract, None, ["jj", "pc0"], ["d256"])
+    ts(T.dg[:], T.yx[:, 0:16], 0.0, None, OP.is_equal, None, ["d256"], ["dg"])
+    ts(T.pc[:, 1:2], T.pc[:, 0:1], 15.0, BIG, OP.is_lt, OP.mult, ["pc0"], ["pc1"])
+    ts(T.dr15[:], T.drp[:], 15, None, OP.bitwise_and, None, ["drp"], ["dr15"])
+    cp(T.drb[:], T.drp[:], ["drp"], ["drb"])
+    cp(T.drc[:], T.dr15[:], ["dr15"], ["drc"])
+
+    def draw_rows(t):
+        for j in range(8 * t, 8 * t + 8):
+            if t:
+                sel(T.ri[:, 128 * j:128 * j + 128], T.one[:], BMP, OP.is_equal, 0.0, -j, 1, ["one"], [("ri", j)])
+            else:
+                ts(T.ri[:, 128 * j:128 * j + 128], T.bm[:], T.dg[:, j:j + 1], None, OP.mult, None, ["bm", "dg"], [("ri", j)])
+
+    def draws_a(t, ka, kb):
+        for i in range(8):
+            j, k, c = 8 * t + i, (ka, kb)[i // 4], 128 * (i % 4)
+            mm(ps[k][:, c:c + 128], T.ri[:, 128 * j:128 * j + 128], T.drc[:], True, True, [("ri", j), "drc"], [("vp", k)], [k])
+        ts(T.pk[:, 256 * t:256 * t + 256], ps[kb][:, 256:512], T.pc[:, 0:1], 16.0, OP.is_le, OP.mult, [("vp", kb), "pc0"], [("pkb", t)], [kb])
+        for k, a, w in ((ka, 768 * t, 512), (kb, 768 * t + 512, 256)):
+            act(T.uu[:, a:a + w], ps[k][:, 0:w], AF.Relu, [("vp", k), "pc4"], [("uu", t, k == kb)], [k], bias=T.pc[:, 4:5], scale=-2.0 ** -17)
+
+    def draws_b(t, ka, kb):
+        for i in range(8):
+            j, k, c = 8 * t + i, (ka, kb)[i // 4], 128 * (i % 4)
+            mm(ps[k][:, c:c + 128], T.ri[:, 128 * j:128 * j + 128], T.drb[:], True, True, [("ri", j), "drb"], [("vp", k)], [k])
+        for k, a, w in ((ka, 768 * t, 512), (kb, 768 * t + 512, 256)):
+            act(T.vv[:, a:a + w], ps[k][:, 0:w], AF.Identity, [("vp", k)], [("vv", t, k == kb)], [k], bias=2.0 ** -18, scale=1.0 / 64)
+        act(ps[5][:, 0:256], ps[kb][:, 256:512], AF.Identity, [("vp", kb)], [("W", 0), ("W", 1)], [kb, 5], bias=1.0, scale=32.0)
+
+    def draws_c(t):
+        p = T.pk[:, 256 * t:256 * t + 256]
+        tt(p, ps[5][:, 0:256], p, OP.add, [("W", 0), ("W", 1), ("pkb", t)], [("pk", t)], [5])
+
+    def codes(lo, hi):
+        for j in range(lo, hi):
+            w = 1 << j
+            act(T.cod[:, w:2 * w], T.cod[:, 0:w], AF.Identity, ["cod", "cb"], ["cod"], bias=T.cb[:, j:j + 1])
+
+    draw_rows(0)
+    act(T.bf1[:], T.bm[:], AF.Copy, ["bm"], ["bf1"])
+    ts(T.cb[:], T.dg[:], 32.0, None, OP.mult, None, ["dg"], ["cb"])
+    ts(T.ta[:, 0:1], T.pc[:, 0:1], 10.5, -16.0, OP.is_lt, OP.mult, ["pc0"], ["ta"])
+    tt(T.cod[:, 0:1], T.ta[:, 0:1], T.dg[:, 11:12], OP.add, ["ta", "dg"], ["cod"])
+    draws_a(0, 2, 3)
+    draws_b(0, 0, 1)
+    codes(0, 8)
+    ts(T.thr[:], T.yx[:], 0.0, -4.0 * BIG, OP.is_le, OP.mult, ["d256"], ["dda"])
+    ts(T.mq[:], T.yx[:], 1.0, BIG, OP.is_equal, OP.mult, ["d256"], ["ddb"])
+    tt(T.dd[:], T.thr[:], T.mq[:], OP.add, ["dda", "ddb"], ["dd"])
+    for w in (128, 256, 512, 1024):
+        cp(T.lk[:, w:2 * w], T.lk[:, 0:w], ["lk"], ["lk"])
+    for k in range(15):
+        ms(T.lk[:, 128 * (k + 1) + k:2048:16], 0.0, [("lkz", k)] if k else ["lk"])
+    LK = ["lk"] + [("lkz", k) for k in range(1, 15)]
+    cp(T.n0u[:], T.n0s[:], ["n0s"], ["n0u"])
+    for h in range(2):
+        cp(T.a1[:, H(h)], T.acs[:].indirect(T.n0u[:, L8(h)]), ["acs", "n0u"], [("a1", h)])
+    ts(T.xm0[:], T.rc[:], 1.0, None, OP.subtract, None, ["rc"], [("xm0", 0), ("xm0", 1)])
+
+    def early(i):
+        if i < 2:
+            o = slice(512 * i, 512 * i + 512)
+            tt(T.da[:, o], T.acs[:, o], T.acn[:, o], OP.subtract, ["acs", "acn"], [("da", i)])
+        if i == 1:
+            ts(T.nb0[:], T.n0s[:], 13.0, 1.0, OP.mult, OP.add, ["n0s"], [("nb0", 0), ("nb0", 1)])
+            draws_c(0)
+        if i == 2:
+            act(T.bf5[:], T.bm[:], AF.Copy, ["bm"], ["bf5"], scale=5.0)
+            ts(T.pc[:, 2:3], T.pc[:, 1:2], 1.0, None, OP.add, None, ["pc1"], ["pc2"])
+            ts(T.pc[:, 3:4], T.pc[:, 1:2], -1.0 / 4096, None, OP.mult, None, ["pc1"], ["pc3"])
+            for t in range(2):
+                ms(T["zl%d" % t][:, 256:272], 0.0, [("zlz", t)])
+            ts(T.t5[:], T.pmi[:], 4, 1, OP.logical_shift_right, OP.bitwise_and, ["pmi"], ["t5x"])
+            cp(T.pc[:, 6:7], T.t5[:, 0:1], ["t5x"], ["pc6"])
+            ts(T.pc[:, 5:6], T.pc[:, 6:7], -1.0, 1.0, OP.mult, OP.add, ["pc6"], ["pc5"])
+            ts(T.b15[:], T.bm[:], T.dg[:, 15:16], None, OP.mult, None, ["bm", "dg"], ["b15"])
+
+    iota(T.n13[:], [[13, 1024]], 3, 0, ["n13"])
+    iota(T.posf0[:], [[-1, 256]], -1, 0, ["posf0"])
+    iota(T.pri0[:], [[16, 16]], 0, 0, ["pri0"])
+    iota(T.dmp[:], [[16, 16]], 2048, 0, ["dmp"])
+    for j in range(8):
+        iota(T.posf1[:, 32 * j:32 * j + 32], [[-1, 32]], -1 - 32 * order[j], 0, [("posf1", j)])
+        iota(T.pri1[:, 2 * j:2 * j + 2], [[16, 2]], 32 * order[j], 0, [("pri1", j)])
+    iota(T.onf[:], [[0, 128]], 1, 0, ["onf"])
+    for t in range(2):
+        iota(T["win%d" % t][:, 0:256], [[0, 256]], 0, 0, [("win", t)])
+    iota(T.rg[:, 2048:2304], [[0, 256]], 0, 0, ["rgd"])
+    D = [[-16, 8], [-1, 16]]
+    for base, f in ((0, 1.0), (-8, 1.0), (1, -1.0), (-7, -1.0)):
+        sel(T.em[:], T.em[:], D, OP.not_equal, f, base, 1, ["em"], ["em"])
+    sel(T.em[:], T.em[:], [[0, 8], [-1, 16]], OP.is_ge, 0.0, 7, 0, ["em"], ["em"])
+    sel(T.em[:], T.em[:], BMP, OP.is_ge, 0.0, 0, 1, ["em"], ["em"])
+    sel(T.em[:], T.em[:], BMQ, OP.is_ge, 0.0, 15, -1, ["em"], ["em"])
+    for k in range(16):
+        sel(T.qm[:], T.qm[:], BMP, OP.not_equal, 32.0 * (pos[k % 8] - (pos[(k + 1) % 8] if k < 15 else 0)), -k, 1, ["qm"], ["qm"])
+    for k in range(8):
+        sel(T.gm[:], T.gm[:], BMP, OP.not_equal, 256.0 * (1 + pos[k]), -k, 1, ["gm"], ["gm"])
+    draw_rows(1)
+
+    def late():
+        ts(T.dz[:], T.idn[:], 16.0, None, OP.mult, None, ["idn"], ["dz"])
+        tt(T.dz[:], T.dz[:], T.bm[:], OP.subtract, ["dz", "bm"], ["dz"])
+        ms(T.cod[:, 2048:2064], 0.0, ["codz"])
+        cp(T.cod[:, 2048:2049], T.dg[:, 11:12], ["dg", "codz"], ["codz"])
+        for n in range(2):
+            pf = [("posf1", j) for j in range(8)] if n else ["posf0"]
+            pr = [("pri1", j) for j in range(8)] if n else ["pri0"]
+            act(T["pos%d" % n][:], T["posf%d" % n][:], AF.Copy, pf + ["dg"], ["pos%d" % n], scale=T.dg[:, 11:12])
+            ts(T["ntr%d" % n][:], T["pri%d" % n][:], T.pc[:, 0:1], -2816.0, OP.add, OP.add, pr + ["pc0"], ["ntr%d" % n])
+            ms(T["dv%d" % n][:], -8192.0, [("dv", n)])
+            ms(T["da%d" % n][:], 0.0, [("dac", n)])
+        ts(T.dmp[:], T.dmp[:], T.pc[:, 0:1], None, OP.add, None, ["dmp", "pc0"], ["dmp"])
+
+    def reach(h, src, key):
+        k = XB[h]
+        mm(ps[k][:, 0:128], T.idn[:], src[:, H(h)], True, False, ["idn", key], [("xp", h)], [k])
+        mm(ps[k][:, 0:128], T.idn[:], T.one[:], False, True, ["idn", "one"], [("xp", h)], [k])
+
+    def records(h, A, key):
+        for s in range(2):
+            c = 2048 * h + 1024 * s
+            act(T.r[:, c:c + 1024], T.rg[:, 0:2048].indirect(A[:, 128 * h + 64 * s:128 * h + 64 * s + 64]), AF.Relu, ["rg", key], [("r", h, s)])
+
+    def mins(h, s, u, uo, ukey):
+        c = 2048 * h + 1024 * s
+        o = slice(64 * s, 64 * s + 64)
+        x = ps[XB[h]][:, o]
+        mm(ps[h][:, o], T.idn[:], u[:, uo + 64 * s:uo + 64 * s + 64], True, False, ["idn", ukey], [("C", h)], [h])
+        for k in range(16):
+            m = T.mn[:, c + 64 * k:c + 64 * k + 64]
+            tt(m, T.r[:, c + k:c + 1024:16], x, OP.min, [("r", h, s), ("xp", h)], [("mn", h, s, k)], [XB[h]])
+            mm(ps[h][:, o], T.lk[:, 128 * k:128 * k + 128], m, False, k == 15, LK + [("mn", h, s, k)], [("C", h)], [h])
+            mm(ps[2 + h][:, o], T.lk[:, 0:128], m, k == 0, k == 15, LK + [("mn", h, s, k)], [("M", h)], [2 + h])
+
+    def choose(h, v, vo, vkey, nu, nukey):
+        tt(T.thr[:, H(h)], ps[2 + h][:, 0:128], v[:, vo:vo + 128], OP.mult, [("M", h), vkey], [("thr", h)], [2 + h])
+        tt(T.b[:, H(h)], ps[h][:, 0:128], T.thr[:, H(h)], OP.is_gt, [("C", h), ("thr", h)], [("b", h)], [h])
+        tt(T.mk[:, H(h)], T.da[:].indirect(nu[:, L8(h)]), T.b[:, H(h)], OP.mult, [("da", 0), ("da", 1), nukey, ("b", h)], [("mk", h)])
+        mm(ps[5][:, H(h)], T.bf1[:], T.mk[:, H(h)], True, True, ["bf1", ("mk", h)], [("W", h)], [5])
+
+    def diag(out, okey, src, skey, h, bk):
+        op("V", lambda e: e.tensor_tensor_scan(out[:, H(h)], T.dd[:, 0:128], src, 0.0, OP.add, OP.max), ["dd", skey], [okey], bk)
+
+    def last(buf, h):
+        return buf[:, 128 * h + 15:128 * h + 128:16]
+
+    def rec_scan(h):
+        diag(T.sc, ("sc", h), ps[5][:, H(h)], ("W", h), h, [5])
+
+    def next_node(h, nb, nbkey):
+        ts(T.t5[:, L8(h)], last(T.sc, h), T.pc[:, 1:2], 5.0, OP.subtract, OP.mult, [("sc", h), "pc1"], [("t5", h)])
+        tt(T.t6[:, L8(h)], T.t5[:, L8(h)], nb[:, L8(h)], OP.add, [("t5", h), nbkey], [("t6", h)])
+        ts(T.ni[:, L8(h)], T.t6[:, L8(h)], 1023, None, OP.bitwise_and, None, [("t6", h)], [("ni", h)])
+        cp(T.nu[:, L8(h)], T.ni[:, L8(h)], [("ni", h)], [("nu", h)])
+
+    def names(h):
+        cp(T.av[:, H(h)], T.acs[:].indirect(T.nu[:, L8(h)]), ["acs", ("nu", h)], [("av", h)])
+
+    def rec_list(h):
+        ts(T.ru[:, L8(h)], last(T.sc, h), T.pc[:, 1:2], None, OP.subtract, None, [("sc", h), "pc1"], [("ru", h)])
+
+    def cut(h, src, skey, dst_, dkey):
+        tt(dst_[:, H(h)], T.pt[:].indirect(T.ru[:, L8(h)]), src[:, H(h)], OP.min, ["pt", ("ru", h), skey], [dkey])
+
+    ranges = [[[(0, 16 * c + 16)] for c in range(16)], []]
+    for c in range(16):
+        q = order[c // 2]
+        a, b2 = sum(1 for p in same if p <= q), sum(1 for p in other if p <= q)
+        ranges[1].append([(o, o + 32 * n) for o, n in ((0, a), (128, b2)) if n])
+    plans = []
+    for n in range(2):
+        size = [sum(b - a for a, b in ranges[n][c]) for c in range(16)]
+        by = sorted(range(16), key=lambda c: size[c])
+        st = []
+        for k, top in ((7, 512), (6, 300)):
+            used = 0
+            while used + size[by[0]] <= top:
+                st.append((by[0], k, used))
+                used += size[by.pop(0)]
+        vt, room = [], [512] * 4
+        for c in reversed(by):
+            k = [k for k in range(4) if room[k] >= size[c]][0]
+            vt.append((c, k, 512 - room[k]))
+            room[k] -= size[c]
+        vt.sort(key=lambda x: (x[1], x[2]))
+        plans.append((size, st, vt))
+
+    def firsts(n, t):
+        o = slice(16 * n, 16 * n + 16)
+        rk = [("recf", n, 0), ("recf", n, 1)]
+        ts(T.ta[:], T.ded[:, o], 2048.0, None, OP.mult, None, [("ded", n, 0), ("ded", n, 1)], ["ta"])
+        tt(T.rw[:], T.recf[:, o], T.ta[:], OP.max, rk + ["ta"], ["rw"])
+        cp(T.rwu[:], T.rw[:], ["rw"], ["rwu"])
+        for j in range(2):
+            ts(T.tin[:, 16 * j:16 * j + 16], T.rw[:], T.pc[:, 5 + j:6 + j], None, OP.mult, None, ["rw", "pc5", "pc6"], [("tin", j)])
+        op("V", lambda e: e.transpose(T.tou[:], T.tin[:]), [("tin", 0), ("tin", 1)], ["tou"])
+        tt(T.tb[:], T.tou[:, 0:16], T.tou[:, 16:32], OP.add, ["tou"], ["tb"])
+        cp(T.rwt[:], T.tb[:], ["tb"], ["rwt"])
+        act(T.cl[:], T.cod[:].indirect(T.rwt[:]), AF.Copy, ["cod", "codz", "rwt"], ["cl"])
+        tt(T.cr[:], T.cod[:].indirect(T.rwu[:]), T["pos%d" % n][:], OP.add, ["cod", "codz", "rwu", "pos%d" % n], ["cr"])
+        for q in range(8):
+            w = T.bdx[:, 256 * q:256 * q + 256]
+            if q < 5:
+                ts(w, T.cl[:], T.bf1[:, 16 * q:16 * q + 1], None, OP.mult, None, ["cl", "bf1"], [("bd", q)])
+            else:
+                act(w, T.cl[:], AF.Copy, ["cl", "bf1"], [("bd", q)], scale=T.bf1[:, 16 * q:16 * q + 1])
+        size, st, vt = plans[n]
+        bdk = [("bd", q) for q in range(8)]
+        if n == 0 and t == 0:
+            draws_a(1, 4, 6)
+        for c, k, a in [x for x in vt if x[1] == 0] + st + [x for x in vt if x[1] != 0]:
+            for lo, hi in ranges[n][c]:
+                mm(ps[k][:, a:a + hi - lo], T.bdx[:, c:2048:16], T.cr[:, lo:hi], True, True, bdk + ["cr"], [("dt", k)], [k])
+                a += hi - lo
+        for c, k, a in st:
+            j = 512 * (k == 6) + a
+            act(T.jk[:, j:j + size[c]], ps[k][:, a:a + size[c]], AF.Relu, [("dt", k), "ntr%d" % n, ("dac", n)], [("jk", n, c), ("dacx", n, c)], [k],
+                bias=T["ntr%d" % n][:, c:c + 1], accum_out=T["da%d" % n][:, c:c + 1])
+        for c, k, a in vt:
+            op("V", lambda e: e.tensor_reduce(T["dv%d" % n][:, c:c + 1], ps[k][:, a:a + size[c]], AxisListType.X, OP.max),
+               [("dt", k), ("dv", n)], [("dvx", n, c)], [k])
+        if st:
+            lastw["jk"] = lastw[("jk", n, st[-1][0])]
+            for c in range(16):
+                lastw[("jk", 1 - n, c)] = lastw["jk"]
+
+    def firsts2(n):
+        o = slice(16 * n, 16 * n + 16)
+        rk = [("recf", n, 0), ("recf", n, 1)]
+        size, st, vt = plans[n]
+        dvk = [("dv", n)] + [("dvx", n, c) for c, _, _ in vt]
+        tt(T.ta[:], T["dv%d" % n][:], T["ntr%d" % n][:], OP.add, dvk + ["ntr%d" % n], ["ta"])
+        tt(T.tb[:], T.ta[:], T["da%d" % n][:], OP.max, ["ta", ("dac", n)] + [("dacx", n, c) for c, _, _ in st], ["tb"])
+        ts(T.ta[:], T.tb[:], 0.0, None, OP.is_gt, None, ["tb"], ["ta"])
+        tt(T.tb[:], T.ta[:], T.ded[:, o], OP.max, ["ta", ("ded", n, 0), ("ded", n, 1)], ["tb"])
+        tt(T.ta[:], T.tb[:], T.dmp[:], OP.mult, ["tb", "dmp"], ["ta"])
+        tt(T.of[:], T.ta[:], T.recf[:, o], OP.max, ["ta"] + rk, ["of"])
+        cp(T.ofu[:, o], T.of[:], ["of"], [("ofu", n)])
+
+    def change(n, z, zk, sign):
+        w = T.rg[:].indirect(T.ofu[:, 16 * n:16 * n + 16])
+        tt(T.ch[:], w, z, sign, ["rg", "rgd", ("ofu", n)] + zk, ["ch"])
+        ts(T.ci[:], T.ch[:], 15.0, -15.0, OP.min, OP.max, ["ch"], ["ci"])
+        cp(w, T.ci[:], ["ci", ("ofu", n)], ["rg", "rgd"])
+
+    mates = [q for q in same if q != me]
+    off = topo.engines(core, T.cores[mates[0]])
+    onc = split([e for e in topo.engines(core, rel[0]) if e not in off], 2)
+
+    def send_relay(buf, key, rbuf, sem):
+        trs = [RemoteDMATransfer(dst_ids=[dst(rel[j], core, topo)], dma_engine_mask=bits(onc[j]), remote_sem=T.sem[sem],
+                                 src=buf[:, 128 + 64 * j:192 + 64 * j], dst=T[rbuf][:, 0:64]) for j in range(2)]
+        nloc[0] += sum(len(x) for x in onc)
+        remote(trs, key)
+
+    def send_same(buf, key, land, sem):
+        trs = []
+        for es, q in zip(share(off, len(mates)), mates):
+            d = T.cores[q]
+            p = places(d, T, topo)[0].index(me)
+            trs.append(RemoteDMATransfer(dst_ids=[dst(d, core, topo)], dma_engine_mask=bits(es), remote_sem=T.sem[sem],
+                                         src=buf[:, 32 * pos[q]:32 * pos[q] + 32], dst=T[land][:, 32 * p:32 * p + 32]))
+            nloc[0] += len(es)
+        remote(trs, key)
+
+    na = nb_ = 0
+    for q in mates:
+        d = T.cores[q]
+        m2 = [x for x in places(d, T, topo)[0] if x != q]
+        na += len(share(topo.engines(d, core), len(m2))[m2.index(me)])
+    for q in other:
+        i = places(T.cores[q], T, topo)[1].index(me)
+        nb_ += len(split(topo.engines(relays(T.cores[q], T, topo)[i // 2], core), 2)[i % 2])
+
+    own = 32 * pos[me]
+    for t in range(2):
+        win, land, zb, zl = T["win%d" % t], T["land%d" % t], T["zb%d" % t], T["zl%d" % t]
+
+        def lev(e, h):
+            o = 256 * (e - 1) + 128 * h
+            return dict(uo=768 * t + o, uk=("uu", t, o >= 512), vk=("vv", t, o >= 512), nu=T.n0u if e == 1 else T.nu,
+                        nk="n0u" if e == 1 else ("nu", h), nb=T.nb0 if e == 1 else T.nb, bk=("nb0", h) if e == 1 else ("nb", h),
+                        x=(T.xm0, T.xm, T.xn)[e - 1], xk=(("xm0", "xm", "xn")[e - 1], h),
+                        x2=(T.xm, T.xn, T.xm)[e - 1], x2k=(("xm", "xn", "xm")[e - 1], h))
+
+        def m_(e, h, s):
+            d = lev(e, h)
+            mins(h, s, T.uu, d["uo"], d["uk"])
+
+        def c_(e, h):
+            d = lev(e, h)
+            choose(h, T.vv, d["uo"], d["vk"], d["nu"], d["nk"])
+
+        def step(e, h):
+            d = lev(e, h)
+            rec_scan(h)
+            rec_list(h)
+            next_node(h, d["nb"], d["bk"])
+            cut(h, d["x"], d["xk"], d["x2"], d["x2k"])
+            names(h)
+            records(h, T.av, ("av", h))
+            reach(h, d["x2"], d["x2k"])
+            if e == 1:
+                ts(T.nb[:, L8(h)], T.ni[:, L8(h)], 13.0, 2.0, OP.mult, OP.add, [("ni", h)], [("nb", h)])
+
+        def way(h):
+            E = ps[7][:, 256 * h + 128:256 * h + 256]
+            mm(E, T.em[:], T.b[:, H(h)], True, True, ["em", ("b", h)], [("E", h)], [7])
+            if h:
+                act(T.mq[:, H(h)], T.n13[:].indirect(T.nu[:, L8(h)]), AF.Copy, ["n13", ("nu", h)], [("mq", h)])
+            else:
+                cp(T.mq[:, H(h)], T.n13[:].indirect(T.nu[:, L8(h)]), ["n13", ("nu", h)], [("mq", h)])
+            ini = T.cum[:, 127:128] if h else 0.0
+            op("V", lambda e: e.tensor_tensor_scan(T.cum[:, H(h)], T.onf[:], E, ini, OP.mult, OP.add),
+               ["onf", ("E", h)] + ([("cum", 0)] if h else []), [("cum", h)], [7])
+            tt(T.ff[:, H(h)], E, T.cum[:, H(h)], OP.mult, [("E", h), ("cum", h)], [("ff", h)], [7])
+            ts(T.gg[:, H(h)], T.ff[:, H(h)], 32.0, None, OP.is_gt, None, [("ff", h)], [("gg", h)])
+            o = slice(256 * h, 256 * h + 128)
+            mm(ps[7][:, o], T.qm[:], T.b[:, H(h)], True, False, ["qm", ("b", h)], [("sl", h)], [7])
+            mm(ps[7][:, o], T.bm[:], T.ff[:, H(h)], False, False, ["bm", ("ff", h)], [("sl", h)], [7])
+            mm(ps[7][:, o], T.gm[:], T.gg[:, H(h)], False, True, ["gm", ("gg", h)], [("sl", h)], [7])
+            k = XB[h]
+            mm(ps[k][:, 128:256], T.bf5[:], T.mk[:, H(h)], True, False, ["bf5", ("mk", h)], [("T", h)], [k])
+            mm(ps[k][:, 128:256], T.b15[:], T.mq[:, H(h)], False, True, ["b15", ("mq", h)], [("T", h)], [k])
+
+        def pack(h):
+            rec_scan(h)
+            rec_list(h)
+            diag(T.ss, ("ssn", h), ps[7][:, 256 * h:256 * h + 128], ("sl", h), h, [7])
+            cut(h, T.xn, ("xn", h), T.xm, ("xm", h))
+            ts(T.su[:, L8(h)], last(T.ss, h), T.pc[:, 2:3], None, OP.subtract, None, [("ssn", h), "pc2"], [("su", h)])
+            ts(T.ti[:, H(h)], ps[XB[h]][:, 128:256], 4096.0, None, OP.mult, None, [("T", h)], [("ti", h)], [XB[h]])
+            ts(T.tj[:, H(h)], T.ti[:, H(h)], 1023 * 4096, None, OP.bitwise_and, None, [("ti", h)], [("tj", h)])
+            p = ps[5][:, 256 + 128 * h:384 + 128 * h]
+            tt(p, T.xm[:, H(h)], T.pk[:, 256 * t + 128 * h:256 * t + 128 * h + 128], OP.add, [("xm", h), ("pk", t)], [("yx", h)], [5])
+            tt(T.y[:, H(h)], T.tj[:, H(h)], p, OP.add, [("tj", h), ("yx", h)], [("y", h)], [5])
+            cp(win[:].indirect(T.su[:, L8(h)]), T.y[:, H(h)], [("su", h), ("y", h)], [("win", t)])
+
+        def lists(h):
+            ts(T.recf[:, L8(h)], last(T.sc, h), T.pc[:, 1:2], None, OP.subtract, None, [("sc", h), "pc1"], [("recf", 0, h)])
+            ts(T.ded[:, L8(h)], last(T.ss, h), T.pc[:, 2:3], 255.5, OP.subtract, OP.is_gt, [("ssn", h), "pc2"], [("ded", 0, h)])
+            ts(T.zo[:, L8(h)], last(T.ss, h), T.pc[:, 2:3], 256.0, OP.subtract, OP.min, [("ssn", h), "pc2"], [("zo", h)])
+
+        for h in range(2):
+            records(h, T.a1, ("a1", h))
+            reach(h, T.xm0, ("xm0", h))
+        if t == 0:
+            early(0)
+        m_(1, 0, 0)
+        if t == 0:
+            early(1)
+        ts(T.pt[:], T.rg[:, 0:2048], 0.0, None, OP.max, None, ["rg"], ["pt"])
+        m_(1, 0, 1)
+        for e in (1, 2, 3):
+            c_(e, 0)
+            if e == 1 and t == 0:
+                early(2)
+            if e == 3:
+                way(0)
+            m_(e, 1, 0)
+            if e < 3:
+                step(e, 0)
+            else:
+                pack(0)
+            m_(e, 1, 1)
+            if e == 3:
+                lists(0)
+            c_(e, 1)
+            if e == 3:
+                way(1)
+            else:
+                m_(e + 1, 0, 0)
+                step(e, 1)
+                if t == 0:
+                    codes(*((8, 10) if e == 1 else (10, 11)))
+                m_(e + 1, 0, 1)
+        pack(1)
+        send_relay(win, [("win", t)], "rl%d" % t, "rq%d" % t)
+        send_same(win, [("win", t)], "land%d" % t, "ha%d" % t)
+        act(land[:, own:own + 32], win[:, own:own + 32], AF.Copy, [("win", t)], [("lown", t)])
+        ext(("lnd", t, 0), "ha%d" % t, na)
+        ext(("lnd", t, 1), "hb%d" % t, nb_)
+        lists(1)
+        if t == 0:
+            late()
+        firsts(0, t)
+
+        def far_in(h):
+            lk = [("lnd", t, h)] + ([] if h else [("lown", t)])
+            op("V", lambda e: e.tensor_tensor_scan(T.ss[:, H(h)], T.dd[:, 0:128], land[:, H(h)], 0.0, OP.add, OP.max), ["dd"] + lk, [("ssn", h)])
+            ts(T.nu[:, L8(h)], last(T.ss, h), 1.0 / 4096, T.pc[:, 3:4], OP.mult, OP.add, [("ssn", h), "pc3"], [("nu", h)])
+            names(h)
+            records(h, T.av, ("av", h))
+            cp(T.yi[:, H(h)], land[:, H(h)], lk, [("yi", h)])
+            ts(T.yj[:, H(h)], T.yi[:, H(h)], 15, None, OP.bitwise_and, None, [("yi", h)], [("yj", h)])
+            cp(ps[XB[h]][:, 0:128], T.yj[:, H(h)], [("yj", h)], [("xp", h)], [XB[h]])
+            ts(T.yk[:, H(h)], T.yi[:, H(h)], 4, 1, OP.logical_shift_right, OP.bitwise_and, [("yi", h)], [("yk", h)])
+            ts(T.u4[:, H(h)], T.yk[:, H(h)], 2.0 ** -13, None, OP.mult, None, [("yk", h)], [("u4", h)])
+            ts(T.yo[:, H(h)], T.yi[:, H(h)], 5, 63, OP.logical_shift_right, OP.bitwise_and, [("yi", h)], [("yo", h)])
+            ts(T.v4[:, H(h)], T.yo[:, H(h)], 1.0 / 64, 2.0 ** -18, OP.mult, OP.add, [("yo", h)], [("v4", h)])
+
+        def far_in2(h):
+            ts(T.xm[:, H(h)], T.yj[:, H(h)], 1.0, None, OP.subtract, None, [("yj", h)], [("xm", h)])
+            cp(T.ni[:, L8(h)], T.nu[:, L8(h)], [("nu", h)], [("ni", h)])
+            ts(T.nb[:, L8(h)], T.ni[:, L8(h)], 13.0, 4.0, OP.mult, OP.add, [("ni", h)], [("nb", h)])
+            ts(T.yl[:, L8(h)], last(T.ss, h), T.pc[:, 1:2], None, OP.subtract, None, [("ssn", h), "pc1"], [("yl", h)])
+            ts(T.ym[:, L8(h)], T.yl[:, L8(h)], 15, None, OP.bitwise_and, None, [("yl", h)], [("ym", h)])
+            ts(T.ded[:, 16 + 8 * h:24 + 8 * h], T.ym[:, L8(h)], 1.0, None, OP.is_lt, None, [("ym", h)], [("ded", 1, h)])
+
+        def leaf(h):
+            E = ps[7][:, 256 * h + 128:256 * h + 256]
+            rec_scan(h)
+            rec_list(h)
+            next_node(h, T.nb, ("nb", h))
+            cut(h, T.xm, ("xm", h), T.xn, ("xn", h))
+            ts(T.xr[:, H(h)], T.xn[:, H(h)], 1.0, None, OP.add, None, [("xn", h)], [("xr", h)])
+            tt(T.val[:, H(h)], T.pys[:].indirect(T.nu[:, L8(h)]), T.xr[:, H(h)], OP.min, ["pys", ("nu", h), ("xr", h)], [("val", h)])
+            mm(E, T.dz[:], T.val[:, H(h)], True, True, ["dz", ("val", h)], [("E", h)], [7])
+            act(zb[:, H(h)], E, AF.Sign, [("E", h)], [("zb", t, h)], [7])
+
+        def far_rec(h):
+            ts(T.recf[:, 16 + 8 * h:24 + 8 * h], last(T.sc, h), T.pc[:, 1:2], None, OP.subtract, None, [("sc", h), "pc1"], [("recf", 1, h)])
+
+        far_in(0)
+        firsts2(0)
+        far_in2(0)
+        mins(0, 0, T.u4, 0, ("u4", 0))
+        far_in(1)
+        mins(0, 1, T.u4, 0, ("u4", 0))
+        choose(0, T.v4, 0, ("v4", 0), T.nu, ("nu", 0))
+        far_in2(1)
+        mins(1, 0, T.u4, 128, ("u4", 1))
+        leaf(0)
+        send_same(zb, [("zb", t, 0)], "zl%d" % t, "za%d" % t)
+        act(zl[:, own:own + 32], zb[:, own:own + 32], AF.Copy, [("zb", t, 0)], [("zown", t)])
+        mins(1, 1, T.u4, 128, ("u4", 1))
+        choose(1, T.v4, 128, ("v4", 1), T.nu, ("nu", 1))
+        far_rec(0)
+        leaf(1)
+        send_relay(zb, [("zb", t, 1)], "rz%d" % t, "rv%d" % t)
+        ext(("zrl", t, 0), "za%d" % t, na)
+        ext(("zrl", t, 1), "zb%d" % t, nb_)
+        far_rec(1)
+        firsts(1, t)
+        firsts2(1)
+        if t == 0:
+            draws_b(1, 4, 6)
+            draws_c(1)
+        change(1, zb[:], [("zb", t, 0), ("zb", t, 1)], OP.add)
+        zk = [("zrl", t, 0), ("zrl", t, 1), ("zown", t), ("zlz", t)]
+        cp(T.zg[:, 0:128], zl[:].indirect(T.zo[:, 0:8]), zk + [("zo", 0)], [("zg", 0)])
+        act(T.zg[:, 128:256], zl[:].indirect(T.zo[:, 8:16]), AF.Copy, zk + [("zo", 1)], [("zg", 1)])
+        change(0, T.zg[:], [("zg", 0), ("zg", 1)], OP.subtract)
+    dma("Y", [(T.yr[:], T.rg[:, 0:2048])], ["rg"], ["yr"])
+    total["loc"] = nloc[0]
+    for s, v in total.items():
+        g.wait_ge(T.sem[s], v)

@@ -64,8 +64,7 @@ def dst(d, src, topo):
 def helper(g, core, home, j, T, topo):
     to = places(home, T, topo)[1][2 * j:2 * j + 2]
     n = 0
-    off = topo.engines(core, T.cores[to[0]])
-    es = split([e for e in topo.engines(home, core) if e not in off], 2)[j]
+    es = split(topo.engines(home, core), 2)[j]
     for t in range(2):
         for arr, buf, land, sem in (("rq", "rl", "land", "hb"), ("rv", "rz", "zl", "zb")):
             g.wait_ge(T.sem["%s%d" % (arr, t)], len(es))
@@ -200,6 +199,19 @@ def rank_program(g, core, T, topo):
         else:
             op("G", lambda e: e.iota(out, pat, base, cm), (), wr)
 
+    def weave(a, b):
+        i = 0
+        for p, f in b:
+            while i < min(p, len(a)):
+                a[i]()
+                i += 1
+            f()
+        for f in a[i:]:
+            f()
+
+    def at(fs, at_):
+        return [(at_[min(i, len(at_) - 1)], f) for i, f in enumerate(fs)]
+
     ps = [T["ps%d" % i] for i in range(8)]
     XB = (4, 6)
     H = lambda h: slice(128 * h, 128 * h + 128)
@@ -300,7 +312,7 @@ def rank_program(g, core, T, topo):
             ts(T.pc[:, 3:4], T.pc[:, 1:2], -1.0 / 4096, None, OP.mult, None, ["pc1"], ["pc3"])
             for t in range(2):
                 ms(T["zl%d" % t][:, 256:272], 0.0, [("zlz", t)])
-            ts(T.t5[:], T.pmi[:], 4, 1, OP.logical_shift_right, OP.bitwise_and, ["pmi"], ["t5x"])
+            ts(T.t5[:], T.pmi[:], 4, 1, OP.logical_shift_right, OP.bitwise_and, ["pmi"], ["t5x", ("t5", 0), ("t5", 1)])
             cp(T.pc[:, 6:7], T.t5[:, 0:1], ["t5x"], ["pc6"])
             ts(T.pc[:, 5:6], T.pc[:, 6:7], -1.0, 1.0, OP.mult, OP.add, ["pc6"], ["pc5"])
             ts(T.b15[:], T.bm[:], T.dg[:, 15:16], None, OP.mult, None, ["bm", "dg"], ["b15"])
@@ -347,27 +359,37 @@ def rank_program(g, core, T, topo):
         mm(ps[k][:, 0:128], T.idn[:], src[:, H(h)], True, False, ["idn", key], [("xp", h)], [k])
         mm(ps[k][:, 0:128], T.idn[:], T.one[:], False, True, ["idn", "one"], [("xp", h)], [k])
 
-    def records(h, A, key):
+    def records(h, A, key, part=False):
         for s in range(2):
             c = 2048 * h + 1024 * s
-            act(T.r[:, c:c + 1024], T.rg[:, 0:2048].indirect(A[:, 128 * h + 64 * s:128 * h + 64 * s + 64]), AF.Relu, ["rg", key], [("r", h, s)])
+            w = T.rg[:, 0:2048]
+            if part and s == 0:
+                act(T.r[:, c:c + 512], w.indirect(A[:, 0:32]), AF.Relu, ["rg", key], [("r", h, s)])
+                ts(T.r[:, c + 512:c + 1024], w.indirect(A[:, 32:64]), 0.0, None, OP.max, None, ["rg", key], [("r2", h, s)])
+            else:
+                act(T.r[:, c:c + 1024], w.indirect(A[:, 128 * h + 64 * s:128 * h + 64 * s + 64]), AF.Relu, ["rg", key], [("r", h, s), ("r2", h, s)])
 
     def mins(h, s, u, uo, ukey):
         c = 2048 * h + 1024 * s
         o = slice(64 * s, 64 * s + 64)
         x = ps[XB[h]][:, o]
-        mm(ps[h][:, o], T.idn[:], u[:, uo + 64 * s:uo + 64 * s + 64], True, False, ["idn", ukey], [("C", h)], [h])
-        for k in range(16):
+
+        def one(k):
+            if k == 0:
+                mm(ps[h][:, o], T.idn[:], u[:, uo + 64 * s:uo + 64 * s + 64], True, False, ["idn", ukey], [("C", h)], [h])
             m = T.mn[:, c + 64 * k:c + 64 * k + 64]
-            tt(m, T.r[:, c + k:c + 1024:16], x, OP.min, [("r", h, s), ("xp", h)], [("mn", h, s, k)], [XB[h]])
+            tt(m, T.r[:, c + k:c + 1024:16], x, OP.min, [("r", h, s), ("r2", h, s), ("xp", h)], [("mn", h, s, k)], [XB[h]])
             mm(ps[h][:, o], T.lk[:, 128 * k:128 * k + 128], m, False, k == 15, LK + [("mn", h, s, k)], [("C", h)], [h])
             mm(ps[2 + h][:, o], T.lk[:, 0:128], m, k == 0, k == 15, LK + [("mn", h, s, k)], [("M", h)], [2 + h])
+        return [lambda k=k: one(k) for k in range(16)]
 
     def choose(h, v, vo, vkey, nu, nukey):
-        tt(T.thr[:, H(h)], ps[2 + h][:, 0:128], v[:, vo:vo + 128], OP.mult, [("M", h), vkey], [("thr", h)], [2 + h])
-        tt(T.b[:, H(h)], ps[h][:, 0:128], T.thr[:, H(h)], OP.is_gt, [("C", h), ("thr", h)], [("b", h)], [h])
-        tt(T.mk[:, H(h)], T.da[:].indirect(nu[:, L8(h)]), T.b[:, H(h)], OP.mult, [("da", 0), ("da", 1), nukey, ("b", h)], [("mk", h)])
-        mm(ps[5][:, H(h)], T.bf1[:], T.mk[:, H(h)], True, True, ["bf1", ("mk", h)], [("W", h)], [5])
+        def mask():
+            tt(T.mk[:, H(h)], T.da[:].indirect(nu[:, L8(h)]), T.b[:, H(h)], OP.mult, [("da", 0), ("da", 1), nukey, ("b", h)], [("mk", h)])
+            mm(ps[5][:, H(h)], T.bf1[:], T.mk[:, H(h)], True, True, ["bf1", ("mk", h)], [("W", h)], [5])
+        return [lambda: tt(T.thr[:, H(h)], ps[2 + h][:, 0:128], v[:, vo:vo + 128], OP.mult, [("M", h), vkey], [("thr", h)], [2 + h]),
+                lambda: tt(T.b[:, H(h)], ps[h][:, 0:128], T.thr[:, H(h)], OP.is_gt, [("C", h), ("thr", h)], [("b", h)], [h]),
+                mask]
 
     def diag(out, okey, src, skey, h, bk):
         op("V", lambda e: e.tensor_tensor_scan(out[:, H(h)], T.dd[:, 0:128], src, 0.0, OP.add, OP.max), ["dd", skey], [okey], bk)
@@ -379,10 +401,11 @@ def rank_program(g, core, T, topo):
         diag(T.sc, ("sc", h), ps[5][:, H(h)], ("W", h), h, [5])
 
     def next_node(h, nb, nbkey):
-        ts(T.t5[:, L8(h)], last(T.sc, h), T.pc[:, 1:2], 5.0, OP.subtract, OP.mult, [("sc", h), "pc1"], [("t5", h)])
-        tt(T.t6[:, L8(h)], T.t5[:, L8(h)], nb[:, L8(h)], OP.add, [("t5", h), nbkey], [("t6", h)])
-        ts(T.ni[:, L8(h)], T.t6[:, L8(h)], 1023, None, OP.bitwise_and, None, [("t6", h)], [("ni", h)])
-        cp(T.nu[:, L8(h)], T.ni[:, L8(h)], [("ni", h)], [("nu", h)])
+        o = L8(h)
+        return [lambda: ts(T.t5[:, o], last(T.sc, h), T.pc[:, 1:2], 5.0, OP.subtract, OP.mult, [("sc", h), "pc1"], [("t5", h)]),
+                lambda: tt(T.t6[:, o], T.t5[:, o], nb[:, o], OP.add, [("t5", h), nbkey], [("t6", h)]),
+                lambda: ts(T.ni[:, o], T.t6[:, o], 1023, None, OP.bitwise_and, None, [("t6", h)], [("ni", h)]),
+                lambda: cp(T.nu[:, o], T.ni[:, o], [("ni", h)], [("nu", h)])]
 
     def names(h):
         cp(T.av[:, H(h)], T.acs[:].indirect(T.nu[:, L8(h)]), ["acs", ("nu", h)], [("av", h)])
@@ -431,7 +454,7 @@ def rank_program(g, core, T, topo):
         tt(T.cr[:], T.cod[:].indirect(T.rwu[:]), T["pos%d" % n][:], OP.add, ["cod", "codz", "rwu", "pos%d" % n], ["cr"])
         for q in range(8):
             w = T.bdx[:, 256 * q:256 * q + 256]
-            if q < 5:
+            if q < 6:
                 ts(w, T.cl[:], T.bf1[:, 16 * q:16 * q + 1], None, OP.mult, None, ["cl", "bf1"], [("bd", q)])
             else:
                 act(w, T.cl[:], AF.Copy, ["cl", "bf1"], [("bd", q)], scale=T.bf1[:, 16 * q:16 * q + 1])
@@ -447,26 +470,28 @@ def rank_program(g, core, T, topo):
             j = 512 * (k == 6) + a
             act(T.jk[:, j:j + size[c]], ps[k][:, a:a + size[c]], AF.Relu, [("dt", k), "ntr%d" % n, ("dac", n)], [("jk", n, c), ("dacx", n, c)], [k],
                 bias=T["ntr%d" % n][:, c:c + 1], accum_out=T["da%d" % n][:, c:c + 1])
+        for c in range(16):
+            lastw[("jk", 1 - n, c)] = lastw[("jk", n, st[-1][0])]
+
+    def most(n):
+        size, st, vt = plans[n]
         for c, k, a in vt:
             op("V", lambda e: e.tensor_reduce(T["dv%d" % n][:, c:c + 1], ps[k][:, a:a + size[c]], AxisListType.X, OP.max),
                [("dt", k), ("dv", n)], [("dvx", n, c)], [k])
-        if st:
-            lastw["jk"] = lastw[("jk", n, st[-1][0])]
-            for c in range(16):
-                lastw[("jk", 1 - n, c)] = lastw["jk"]
 
     def firsts2(n):
         o = slice(16 * n, 16 * n + 16)
         rk = [("recf", n, 0), ("recf", n, 1)]
         size, st, vt = plans[n]
         dvk = [("dv", n)] + [("dvx", n, c) for c, _, _ in vt]
-        tt(T.ta[:], T["dv%d" % n][:], T["ntr%d" % n][:], OP.add, dvk + ["ntr%d" % n], ["ta"])
-        tt(T.tb[:], T.ta[:], T["da%d" % n][:], OP.max, ["ta", ("dac", n)] + [("dacx", n, c) for c, _, _ in st], ["tb"])
-        ts(T.ta[:], T.tb[:], 0.0, None, OP.is_gt, None, ["tb"], ["ta"])
-        tt(T.tb[:], T.ta[:], T.ded[:, o], OP.max, ["ta", ("ded", n, 0), ("ded", n, 1)], ["tb"])
-        tt(T.ta[:], T.tb[:], T.dmp[:], OP.mult, ["tb", "dmp"], ["ta"])
-        tt(T.of[:], T.ta[:], T.recf[:, o], OP.max, ["ta"] + rk, ["of"])
-        cp(T.ofu[:, o], T.of[:], ["of"], [("ofu", n)])
+        return [
+            lambda: tt(T.ta[:], T["dv%d" % n][:], T["ntr%d" % n][:], OP.add, dvk + ["ntr%d" % n], ["ta"]),
+            lambda: tt(T.tb[:], T.ta[:], T["da%d" % n][:], OP.max, ["ta", ("dac", n)] + [("dacx", n, c) for c, _, _ in st], ["tb"]),
+            lambda: ts(T.ta[:], T.tb[:], 0.0, None, OP.is_gt, None, ["tb"], ["ta"]),
+            lambda: tt(T.tb[:], T.ta[:], T.ded[:, o], OP.max, ["ta", ("ded", n, 0), ("ded", n, 1)], ["tb"]),
+            lambda: tt(T.ta[:], T.tb[:], T.dmp[:], OP.mult, ["tb", "dmp"], ["ta"]),
+            lambda: tt(T.of[:], T.ta[:], T.recf[:, o], OP.max, ["ta"] + rk, ["of"]),
+            lambda: cp(T.ofu[:, o], T.of[:], ["of"], [("ofu", n)])]
 
     def change(n, z, zk, sign):
         w = T.rg[:].indirect(T.ofu[:, 16 * n:16 * n + 16])
@@ -476,7 +501,7 @@ def rank_program(g, core, T, topo):
 
     mates = [q for q in same if q != me]
     off = topo.engines(core, T.cores[mates[0]])
-    onc = split([e for e in topo.engines(core, rel[0]) if e not in off], 2)
+    onc = split(topo.engines(core, rel[0]), 2)
 
     def send_relay(buf, key, rbuf, sem):
         trs = [RemoteDMATransfer(dst_ids=[dst(rel[j], core, topo)], dma_engine_mask=bits(onc[j]), remote_sem=T.sem[sem],
@@ -504,6 +529,7 @@ def rank_program(g, core, T, topo):
         nb_ += len(split(topo.engines(relays(T.cores[q], T, topo)[i // 2], core), 2)[i % 2])
 
     own = 32 * pos[me]
+    CP, SP, WP, KP = (0, 2, 4), (8, 9, 11, 12, 14, 15, 16, 21, 23, 25, 27), (6, 8, 10, 12), range(15, 25)
     for t in range(2):
         win, land, zb, zl = T["win%d" % t], T["land%d" % t], T["zb%d" % t], T["zl%d" % t]
 
@@ -514,58 +540,66 @@ def rank_program(g, core, T, topo):
                         x=(T.xm0, T.xm, T.xn)[e - 1], xk=(("xm0", "xm", "xn")[e - 1], h),
                         x2=(T.xm, T.xn, T.xm)[e - 1], x2k=(("xm", "xn", "xm")[e - 1], h))
 
-        def m_(e, h, s):
+        def m_(e, h):
             d = lev(e, h)
-            mins(h, s, T.uu, d["uo"], d["uk"])
+            return mins(h, 0, T.uu, d["uo"], d["uk"]) + mins(h, 1, T.uu, d["uo"], d["uk"])
 
         def c_(e, h):
             d = lev(e, h)
-            choose(h, T.vv, d["uo"], d["vk"], d["nu"], d["nk"])
+            return choose(h, T.vv, d["uo"], d["vk"], d["nu"], d["nk"])
 
         def step(e, h):
             d = lev(e, h)
-            rec_scan(h)
-            rec_list(h)
-            next_node(h, d["nb"], d["bk"])
-            cut(h, d["x"], d["xk"], d["x2"], d["x2k"])
-            names(h)
-            records(h, T.av, ("av", h))
-            reach(h, d["x2"], d["x2k"])
+            nn = next_node(h, d["nb"], d["bk"])
+
+            def go():
+                names(h)
+                records(h, T.av, ("av", h))
+            r = [lambda: rec_scan(h), nn[0], lambda: rec_list(h)] + nn[1:] + [go, lambda: cut(h, d["x"], d["xk"], d["x2"], d["x2k"]),
+                 lambda: reach(h, d["x2"], d["x2k"])]
             if e == 1:
-                ts(T.nb[:, L8(h)], T.ni[:, L8(h)], 13.0, 2.0, OP.mult, OP.add, [("ni", h)], [("nb", h)])
+                r.append(lambda: ts(T.nb[:, L8(h)], T.ni[:, L8(h)], 13.0, 2.0, OP.mult, OP.add, [("ni", h)], [("nb", h)]))
+            if t == 0 and h:
+                r.append(lambda: codes(*((8, 10) if e == 1 else (10, 11))))
+            return r
 
         def way(h):
-            E = ps[7][:, 256 * h + 128:256 * h + 256]
-            mm(E, T.em[:], T.b[:, H(h)], True, True, ["em", ("b", h)], [("E", h)], [7])
-            if h:
-                act(T.mq[:, H(h)], T.n13[:].indirect(T.nu[:, L8(h)]), AF.Copy, ["n13", ("nu", h)], [("mq", h)])
-            else:
-                cp(T.mq[:, H(h)], T.n13[:].indirect(T.nu[:, L8(h)]), ["n13", ("nu", h)], [("mq", h)])
+            E, o, k = ps[7][:, 256 * h + 128:256 * h + 256], slice(256 * h, 256 * h + 128), XB[h]
             ini = T.cum[:, 127:128] if h else 0.0
-            op("V", lambda e: e.tensor_tensor_scan(T.cum[:, H(h)], T.onf[:], E, ini, OP.mult, OP.add),
-               ["onf", ("E", h)] + ([("cum", 0)] if h else []), [("cum", h)], [7])
-            tt(T.ff[:, H(h)], E, T.cum[:, H(h)], OP.mult, [("E", h), ("cum", h)], [("ff", h)], [7])
-            ts(T.gg[:, H(h)], T.ff[:, H(h)], 32.0, None, OP.is_gt, None, [("ff", h)], [("gg", h)])
-            o = slice(256 * h, 256 * h + 128)
-            mm(ps[7][:, o], T.qm[:], T.b[:, H(h)], True, False, ["qm", ("b", h)], [("sl", h)], [7])
-            mm(ps[7][:, o], T.bm[:], T.ff[:, H(h)], False, False, ["bm", ("ff", h)], [("sl", h)], [7])
-            mm(ps[7][:, o], T.gm[:], T.gg[:, H(h)], False, True, ["gm", ("gg", h)], [("sl", h)], [7])
-            k = XB[h]
-            mm(ps[k][:, 128:256], T.bf5[:], T.mk[:, H(h)], True, False, ["bf5", ("mk", h)], [("T", h)], [k])
-            mm(ps[k][:, 128:256], T.b15[:], T.mq[:, H(h)], False, True, ["b15", ("mq", h)], [("T", h)], [k])
+
+            def a():
+                mm(E, T.em[:], T.b[:, H(h)], True, True, ["em", ("b", h)], [("E", h)], [7])
+                if h:
+                    act(T.mq[:, H(h)], T.n13[:].indirect(T.nu[:, L8(h)]), AF.Copy, ["n13", ("nu", h)], [("mq", h)])
+                else:
+                    cp(T.mq[:, H(h)], T.n13[:].indirect(T.nu[:, L8(h)]), ["n13", ("nu", h)], [("mq", h)])
+
+            def b():
+                op("V", lambda e: e.tensor_tensor_scan(T.cum[:, H(h)], T.onf[:], E, ini, OP.mult, OP.add),
+                   ["onf", ("E", h)] + ([("cum", 0)] if h else []), [("cum", h)], [7])
+
+            def d():
+                ts(T.gg[:, H(h)], T.ff[:, H(h)], 32.0, None, OP.is_gt, None, [("ff", h)], [("gg", h)])
+                mm(ps[7][:, o], T.qm[:], T.b[:, H(h)], True, False, ["qm", ("b", h)], [("sl", h)], [7])
+                mm(ps[7][:, o], T.bm[:], T.ff[:, H(h)], False, False, ["bm", ("ff", h)], [("sl", h)], [7])
+                mm(ps[7][:, o], T.gm[:], T.gg[:, H(h)], False, True, ["gm", ("gg", h)], [("sl", h)], [7])
+                mm(ps[k][:, 128:256], T.bf5[:], T.mk[:, H(h)], True, False, ["bf5", ("mk", h)], [("T", h)], [k])
+                mm(ps[k][:, 128:256], T.b15[:], T.mq[:, H(h)], False, True, ["b15", ("mq", h)], [("T", h)], [k])
+            return [a, b, lambda: tt(T.ff[:, H(h)], E, T.cum[:, H(h)], OP.mult, [("E", h), ("cum", h)], [("ff", h)], [7]), d]
 
         def pack(h):
-            rec_scan(h)
-            rec_list(h)
-            diag(T.ss, ("ssn", h), ps[7][:, 256 * h:256 * h + 128], ("sl", h), h, [7])
-            cut(h, T.xn, ("xn", h), T.xm, ("xm", h))
-            ts(T.su[:, L8(h)], last(T.ss, h), T.pc[:, 2:3], None, OP.subtract, None, [("ssn", h), "pc2"], [("su", h)])
-            ts(T.ti[:, H(h)], ps[XB[h]][:, 128:256], 4096.0, None, OP.mult, None, [("T", h)], [("ti", h)], [XB[h]])
-            ts(T.tj[:, H(h)], T.ti[:, H(h)], 1023 * 4096, None, OP.bitwise_and, None, [("ti", h)], [("tj", h)])
-            p = ps[5][:, 256 + 128 * h:384 + 128 * h]
-            tt(p, T.xm[:, H(h)], T.pk[:, 256 * t + 128 * h:256 * t + 128 * h + 128], OP.add, [("xm", h), ("pk", t)], [("yx", h)], [5])
-            tt(T.y[:, H(h)], T.tj[:, H(h)], p, OP.add, [("tj", h), ("yx", h)], [("y", h)], [5])
-            cp(win[:].indirect(T.su[:, L8(h)]), T.y[:, H(h)], [("su", h), ("y", h)], [("win", t)])
+            p, k = ps[5][:, 256 + 128 * h:384 + 128 * h], XB[h]
+            return [
+                lambda: rec_scan(h),
+                lambda: rec_list(h),
+                lambda: diag(T.ss, ("ssn", h), ps[7][:, 256 * h:256 * h + 128], ("sl", h), h, [7]),
+                lambda: cut(h, T.xn, ("xn", h), T.xm, ("xm", h)),
+                lambda: ts(T.su[:, L8(h)], last(T.ss, h), T.pc[:, 2:3], None, OP.subtract, None, [("ssn", h), "pc2"], [("su", h)]),
+                lambda: ts(T.ti[:, H(h)], ps[k][:, 128:256], 4096.0, None, OP.mult, None, [("T", h)], [("ti", h)], [k]),
+                lambda: tt(p, T.xm[:, H(h)], T.pk[:, 256 * t + 128 * h:256 * t + 128 * h + 128], OP.add, [("xm", h), ("pk", t)], [("yx", h)], [5]),
+                lambda: ts(T.tj[:, H(h)], T.ti[:, H(h)], 1023 * 4096, None, OP.bitwise_and, None, [("ti", h)], [("tj", h)]),
+                lambda: tt(T.y[:, H(h)], T.tj[:, H(h)], p, OP.add, [("tj", h), ("yx", h)], [("y", h)], [5]),
+                lambda: cp(win[:].indirect(T.su[:, L8(h)]), T.y[:, H(h)], [("su", h), ("y", h)], [("win", t)])]
 
         def lists(h):
             ts(T.recf[:, L8(h)], last(T.sc, h), T.pc[:, 1:2], None, OP.subtract, None, [("sc", h), "pc1"], [("recf", 0, h)])
@@ -573,39 +607,24 @@ def rank_program(g, core, T, topo):
             ts(T.zo[:, L8(h)], last(T.ss, h), T.pc[:, 2:3], 256.0, OP.subtract, OP.min, [("ssn", h), "pc2"], [("zo", h)])
 
         for h in range(2):
-            records(h, T.a1, ("a1", h))
+            records(h, T.a1, ("a1", h), h == 0)
             reach(h, T.xm0, ("xm0", h))
         if t == 0:
             early(0)
-        m_(1, 0, 0)
+        r = m_(1, 0)
         if t == 0:
-            early(1)
-        ts(T.pt[:], T.rg[:, 0:2048], 0.0, None, OP.max, None, ["rg"], ["pt"])
-        m_(1, 0, 1)
-        for e in (1, 2, 3):
-            c_(e, 0)
-            if e == 1 and t == 0:
-                early(2)
-            if e == 3:
-                way(0)
-            m_(e, 1, 0)
-            if e < 3:
-                step(e, 0)
-            else:
-                pack(0)
-            m_(e, 1, 1)
-            if e == 3:
-                lists(0)
-            c_(e, 1)
-            if e == 3:
-                way(1)
-            else:
-                m_(e + 1, 0, 0)
-                step(e, 1)
-                if t == 0:
-                    codes(*((8, 10) if e == 1 else (10, 11)))
-                m_(e + 1, 0, 1)
-        pack(1)
+            r.insert(16, lambda: early(1))
+        r.insert(17, lambda: ts(T.pt[:], T.rg[:, 0:2048], 0.0, None, OP.max, None, ["rg"], ["pt"]))
+        for f in r:
+            f()
+        for e in (1, 2):
+            x = at([lambda: early(2)], (14,)) if e == 1 and t == 0 else []
+            weave(m_(e, 1), at(c_(e, 0), CP) + x + at(step(e, 0), SP))
+            weave(m_(e + 1, 0), at(c_(e, 1), CP) + at(step(e, 1), SP))
+        weave(m_(3, 1), at(c_(3, 0), CP) + at(way(0), WP) + at(pack(0), KP))
+        lists(0)
+        for f in c_(3, 1) + way(1) + pack(1):
+            f()
         send_relay(win, [("win", t)], "rl%d" % t, "rq%d" % t)
         send_same(win, [("win", t)], "land%d" % t, "ha%d" % t)
         act(land[:, own:own + 32], win[:, own:own + 32], AF.Copy, [("win", t)], [("lown", t)])
@@ -627,53 +646,53 @@ def rank_program(g, core, T, topo):
             cp(ps[XB[h]][:, 0:128], T.yj[:, H(h)], [("yj", h)], [("xp", h)], [XB[h]])
             ts(T.yk[:, H(h)], T.yi[:, H(h)], 4, 1, OP.logical_shift_right, OP.bitwise_and, [("yi", h)], [("yk", h)])
             ts(T.u4[:, H(h)], T.yk[:, H(h)], 2.0 ** -13, None, OP.mult, None, [("yk", h)], [("u4", h)])
-            ts(T.yo[:, H(h)], T.yi[:, H(h)], 5, 63, OP.logical_shift_right, OP.bitwise_and, [("yi", h)], [("yo", h)])
-            ts(T.v4[:, H(h)], T.yo[:, H(h)], 1.0 / 64, 2.0 ** -18, OP.mult, OP.add, [("yo", h)], [("v4", h)])
 
         def far_in2(h):
-            ts(T.xm[:, H(h)], T.yj[:, H(h)], 1.0, None, OP.subtract, None, [("yj", h)], [("xm", h)])
-            cp(T.ni[:, L8(h)], T.nu[:, L8(h)], [("nu", h)], [("ni", h)])
-            ts(T.nb[:, L8(h)], T.ni[:, L8(h)], 13.0, 4.0, OP.mult, OP.add, [("ni", h)], [("nb", h)])
-            ts(T.yl[:, L8(h)], last(T.ss, h), T.pc[:, 1:2], None, OP.subtract, None, [("ssn", h), "pc1"], [("yl", h)])
-            ts(T.ym[:, L8(h)], T.yl[:, L8(h)], 15, None, OP.bitwise_and, None, [("yl", h)], [("ym", h)])
-            ts(T.ded[:, 16 + 8 * h:24 + 8 * h], T.ym[:, L8(h)], 1.0, None, OP.is_lt, None, [("ym", h)], [("ded", 1, h)])
+            a = L8(h)
+            return [
+                lambda: ts(T.yo[:, H(h)], T.yi[:, H(h)], 5, 63, OP.logical_shift_right, OP.bitwise_and, [("yi", h)], [("yo", h)]),
+                lambda: ts(T.v4[:, H(h)], T.yo[:, H(h)], 1.0 / 64, 2.0 ** -18, OP.mult, OP.add, [("yo", h)], [("v4", h)]),
+                lambda: ts(T.xm[:, H(h)], T.yj[:, H(h)], 1.0, None, OP.subtract, None, [("yj", h)], [("xm", h)]),
+                lambda: cp(T.ni[:, a], T.nu[:, a], [("nu", h)], [("ni", h)]),
+                lambda: ts(T.nb[:, a], T.ni[:, a], 13.0, 4.0, OP.mult, OP.add, [("ni", h)], [("nb", h)]),
+                lambda: ts(T.yl[:, a], last(T.ss, h), T.pc[:, 1:2], None, OP.subtract, None, [("ssn", h), "pc1"], [("yl", h)]),
+                lambda: ts(T.ym[:, a], T.yl[:, a], 15, None, OP.bitwise_and, None, [("yl", h)], [("ym", h)]),
+                lambda: ts(T.ded[:, 16 + 8 * h:24 + 8 * h], T.ym[:, a], 1.0, None, OP.is_lt, None, [("ym", h)], [("ded", 1, h)])]
 
         def leaf(h):
             E = ps[7][:, 256 * h + 128:256 * h + 256]
-            rec_scan(h)
-            rec_list(h)
-            next_node(h, T.nb, ("nb", h))
-            cut(h, T.xm, ("xm", h), T.xn, ("xn", h))
-            ts(T.xr[:, H(h)], T.xn[:, H(h)], 1.0, None, OP.add, None, [("xn", h)], [("xr", h)])
-            tt(T.val[:, H(h)], T.pys[:].indirect(T.nu[:, L8(h)]), T.xr[:, H(h)], OP.min, ["pys", ("nu", h), ("xr", h)], [("val", h)])
-            mm(E, T.dz[:], T.val[:, H(h)], True, True, ["dz", ("val", h)], [("E", h)], [7])
-            act(zb[:, H(h)], E, AF.Sign, [("E", h)], [("zb", t, h)], [7])
+            nn = next_node(h, T.nb, ("nb", h))
 
-        def far_rec(h):
-            ts(T.recf[:, 16 + 8 * h:24 + 8 * h], last(T.sc, h), T.pc[:, 1:2], None, OP.subtract, None, [("sc", h), "pc1"], [("recf", 1, h)])
+            def sign():
+                tt(T.val[:, H(h)], T.pys[:].indirect(T.nu[:, L8(h)]), T.xr[:, H(h)], OP.min, ["pys", ("nu", h), ("xr", h)], [("val", h)])
+                mm(E, T.dz[:], T.val[:, H(h)], True, True, ["dz", ("val", h)], [("E", h)], [7])
+                act(zb[:, H(h)], E, AF.Sign, [("E", h)], [("zb", t, h)], [7])
+                if h:
+                    send_relay(zb, [("zb", t, 1)], "rz%d" % t, "rv%d" % t)
+                else:
+                    send_same(zb, [("zb", t, 0)], "zl%d" % t, "za%d" % t)
+                    act(zl[:, own:own + 32], zb[:, own:own + 32], AF.Copy, [("zb", t, 0)], [("zown", t)])
+
+            return [lambda: rec_scan(h), nn[0], lambda: rec_list(h), nn[1], nn[2], lambda: cut(h, T.xm, ("xm", h), T.xn, ("xn", h)), nn[3],
+                    lambda: ts(T.xr[:, H(h)], T.xn[:, H(h)], 1.0, None, OP.add, None, [("xn", h)], [("xr", h)]), sign,
+                    lambda: ts(T.recf[:, 16 + 8 * h:24 + 8 * h], last(T.sc, h), T.pc[:, 1:2], None, OP.subtract, None, [("sc", h), "pc1"], [("recf", 1, h)])]
 
         far_in(0)
-        firsts2(0)
-        far_in2(0)
-        mins(0, 0, T.u4, 0, ("u4", 0))
-        far_in(1)
-        mins(0, 1, T.u4, 0, ("u4", 0))
-        choose(0, T.v4, 0, ("v4", 0), T.nu, ("nu", 0))
-        far_in2(1)
-        mins(1, 0, T.u4, 128, ("u4", 1))
-        leaf(0)
-        send_same(zb, [("zb", t, 0)], "zl%d" % t, "za%d" % t)
-        act(zl[:, own:own + 32], zb[:, own:own + 32], AF.Copy, [("zb", t, 0)], [("zown", t)])
-        mins(1, 1, T.u4, 128, ("u4", 1))
-        choose(1, T.v4, 128, ("v4", 1), T.nu, ("nu", 1))
-        far_rec(0)
-        leaf(1)
-        send_relay(zb, [("zb", t, 1)], "rz%d" % t, "rv%d" % t)
+        most(0)
+        m4 = [mins(h, 0, T.u4, 128 * h, ("u4", h)) + mins(h, 1, T.u4, 128 * h, ("u4", h)) for h in range(2)]
+        c4 = [choose(h, T.v4, 128 * h, ("v4", h), T.nu, ("nu", h)) for h in range(2)]
+        a, b = far_in2(0), firsts2(0)
+        mix = [f for p in zip(a, b) for f in p] + a[len(b):]
+        weave(m4[0], sorted(at(mix, (0, 0, 0, 2, 4, 6, 8, 10, 12, 14, 15)) + [(14, lambda: far_in(1))] + at(far_in2(1), range(18, 26)), key=lambda x: x[0]))
+        weave(m4[1], at(c4[0], CP) + at(leaf(0), SP))
+        for f in c4[1] + leaf(1):
+            f()
         ext(("zrl", t, 0), "za%d" % t, na)
         ext(("zrl", t, 1), "zb%d" % t, nb_)
-        far_rec(1)
         firsts(1, t)
-        firsts2(1)
+        most(1)
+        for f in firsts2(1):
+            f()
         if t == 0:
             draws_b(1, 4, 6)
             draws_c(1)

from concourse.bass import DstId, RemoteDMATransfer
from concourse.mybir import AluOpType as OP, AxisListType, ActivationFunctionType as AF

BIG = float(1 << 22)
F4, B2, I4, U2 = "float32", "bfloat16", "int32", "uint16"
SCRATCH = {}
for _d, _w, _s in (
        (I4, 1024, "acs acn"), (F4, 1024, "da n13"), (B2, 2304, "rg"), (B2, 1024, "pys jk"), (B2, 256, "rc"), (I4, 16, "n0s"),
        (I4, 128, "drp dr15"), (B2, 128, "drb drc one bm idn dz em qm gm"), (F4, 128, "bf1 bf5 b15 onf"), (B2, 2048, "lk ri bdx pt"),
        (I4, 16, "pmi pma"), (I4, 256, "jj"), (F4, 8, "pc"), (F4, 16, "dg"), (F4, 256, "dd"), (B2, 2064, "cod"), (B2, 16, "cb"),
        (F4, 16, "ta tb rw of pri0 pri1 ntr0 ntr1 dmp dv0 dv1 da0 da1"), (F4, 32, "tin tou recf ded"), (F4, 256, "posf0 posf1"),
        (B2, 256, "pos0 pos1 xm0 xm xn xr b ff gg u4 val zb0 zb1 zg cl cr ch ci"), (F4, 1536, "vv"), (B2, 1536, "uu"), (F4, 512, "pk"),
        (U2, 16, "n0u nu ru su zo rwu rwt"), (I4, 16, "nb0 ni nb t5 t6 yl ym"), (U2, 256, "a1 av"), (U2, 32, "ofu"), (B2, 4096, "r mn"),
        (F4, 256, "thr mk mq sc ss cum y yx land0 land1 v4"), (I4, 256, "ti tj yi yj yk yo"), (F4, 2560, "win0 win1"),
        (B2, 272, "zl0 zl1"), (F4, 64, "rl0 rl1"), (B2, 64, "rz0 rz1")):
    for _n in _s.split():
        SCRATCH[_n] = ("sbuf", [128, _w], _d)
for _n in range(8):
    SCRATCH["ps%d" % _n] = ("psum", [128, 512], F4)
SEMAPHORES = ["sv", "ss", "sp", "sg", "loc"] + ["ld%d" % _i for _i in range(12)] + \
    ["%s%d" % (_a, _t) for _a in ("ha", "hb", "za", "zb", "rq", "rv") for _t in range(2)]


def bits(es):
    m = 0
    for e in es:
        m |= 1 << e
    return m


def split(es, n):
    w = len(es) // n
    return [es[j * w:(j + 1) * w] for j in range(n)]


def share(es, n):
    out, left = [], list(es)
    for j in range(n, 0, -1):
        w = 1
        while w * 2 * j <= len(left):
            w *= 2
        out.append(left[:w])
        left = left[w:]
    return out


def places(core, T, topo):
    same = [q for q in range(8) if T.cores[q] == core or topo.may_write(core, T.cores[q])]
    return same, [q for q in range(8) if q not in same]


def relays(core, T, topo):
    other = places(core, T, topo)[1]
    c = [d for d in topo.cores_of(core) if d != core and all(topo.may_write(d, T.cores[q]) for q in other)]
    c.sort(key=lambda d: (topo.die(d) != topo.die(core), d))
    return c[:2]


def dst(d, src, topo):
    rid, pid = topo.addr(d, src)
    return DstId(rid=rid, pnc=pid)


def helper(g, core, home, j, T, topo):
    to = places(home, T, topo)[1][2 * j:2 * j + 2]
    n = 0
    es = split(topo.engines(home, core), 2)[j]
    for t in range(2):
        for arr, buf, land, sem in (("rq", "rl", "land", "hb"), ("rv", "rz", "zl", "zb")):
            g.wait_ge(T.sem["%s%d" % (arr, t)], len(es))
            trs = []
            for i, q in enumerate(to):
                d = T.cores[q]
                s2, o2 = places(d, T, topo)
                p = (s2 + o2).index(T.rank_of(home))
                ee = split(topo.engines(core, d), 2)[i]
                trs.append(RemoteDMATransfer(dst_ids=[dst(d, core, topo)], dma_engine_mask=bits(ee), remote_sem=T.sem["%s%d" % (sem, t)],
                                             src=T["%s%d" % (buf, t)][:, 32 * i:32 * i + 32], dst=T["%s%d" % (land, t)][:, 32 * p:32 * p + 32]))
                n += len(ee)
            g.remote_dma_fused(trs, local_sem=T.sem.loc)
    g.wait_ge(T.sem.loc, n)


def rank_program(g, core, T, topo):
    me = T.rank_of(core)
    if me is None:
        for c in T.cores:
            rel = relays(c, T, topo)
            if core in rel:
                helper(g, core, c, rel.index(core), T, topo)
        return
    same, other = places(core, T, topo)
    order = same + other
    pos = [order.index(q) for q in range(8)]
    rel = relays(core, T, topo)

    Q = {"V": g.vector, "S": g.scalar, "P": g.tensor, "G": g, "Y": g.sync}
    SEM = {"V": "sv", "S": "ss", "P": "sp", "G": "sg"}
    total, known, clocks = {}, {q: {} for q in Q}, {}
    lastw, readers, bank = {}, {}, {}
    nld, nloc = [0], [0]

    def merge(a, b):
        for k, v in b.items():
            if a.get(k, 0) < v:
                a[k] = v

    def waits(q, unit, rd, wr, bk):
        need = {}

        def add(tok):
            _, s, v = tok
            if known[q].get(s, 0) < v and need.get(s, 0) < v:
                need[s] = v
        for k in rd:
            if k in lastw:
                add(lastw[k])
        for k in wr:
            if k in lastw and (lastw[k][0] != unit or unit != "P"):
                add(lastw[k])
            for u2, tok in readers.get(k, {}).items():
                if u2 != unit:
                    add(tok)
        for k in bk:
            for u2, tok in bank.get(k, {}).items():
                if u2 != unit:
                    add(tok)
        items = list(need.items())
        for s, v in items:
            if not any(s2 != s and clocks[(s2, v2)].get(s, 0) >= v for s2, v2 in items):
                Q[q].wait_ge(T.sem[s], v)
        for s, v in items:
            merge(known[q], clocks[(s, v)])

    def note(q, unit, tok, rd, wr, bk):
        c = dict(known[q])
        merge(c, {tok[1]: tok[2]})
        clocks[(tok[1], tok[2])] = c
        for k in rd:
            readers.setdefault(k, {})[unit] = tok
        for k in wr:
            lastw[k] = tok
            readers[k] = {}
        for k in bk:
            bank.setdefault(k, {})[unit] = tok

    def op(q, fn, rd, wr, bk=()):
        waits(q, q, rd, wr, bk)
        s = SEM[q]
        total[s] = total.get(s, 0) + 1
        fn(Q[q]).then_inc(T.sem[s], 1)
        note(q, q, (q, s, total[s]), rd, wr, bk)

    def dma(q, pairs, rd, wr):
        s = "ld%d" % nld[0]
        nld[0] += 1
        waits(q, s, rd, wr, ())
        for o, i in pairs:
            Q[q].dma_start(o, i).then_inc(T.sem[s], 16)
        total[s] = 16 * len(pairs)
        note(q, s, (s, s, total[s]), rd, wr, ())

    def ext(k, s, v):
        total[s] = v
        clocks[(s, v)] = {s: v}
        lastw[k] = ("X", s, v)

    def remote(trs, rd):
        waits("G", "R", rd, (), ())
        g.remote_dma_fused(trs, local_sem=T.sem.loc)

    def tt(out, a, b_, o, rd, wr, bk=()):
        op("V", lambda e: e.tensor_tensor(out, a, b_, o), rd, wr, bk)

    def ts(out, a, s1, s2, o1, o2, rd, wr, bk=()):
        if o2 is None:
            op("V", lambda e: e.tensor_scalar(out, a, s1, None, o1), rd, wr, bk)
        else:
            op("V", lambda e: e.tensor_scalar(out, a, s1, s2, o1, o2), rd, wr, bk)

    def cp(out, a, rd, wr, bk=()):
        op("V", lambda e: e.tensor_copy(out, a), rd, wr, bk)

    def ms(ap, c, wr):
        op("V", lambda e: e.memset(ap, c), (), wr)

    def act(out, a, f, rd, wr, bk=(), **kw):
        op("S", lambda e: e.activation(out, a, f, **kw), rd, wr, bk)

    def mm(out, l, r_, st, sp, rd, wr, bk):
        op("P", lambda e: e.matmul(out, l, r_, st, sp), rd, wr, bk)

    def sel(out, a, pat, o, fill, base, cm, rd, wr):
        op("G", lambda e: e.affine_select(out, a, pat, o, fill, base, cm), rd, wr)

    def iota(out, pat, base, cm, wr, flag=True):
        if flag:
            op("G", lambda e: e.iota(out, pat, base, cm, allow_small_or_imprecise_dtypes=True), (), wr)
        else:
            op("G", lambda e: e.iota(out, pat, base, cm), (), wr)

    def weave(a, b):
        i = 0
        for p, f in b:
            while i < min(p, len(a)):
                a[i]()
                i += 1
            f()
        for f in a[i:]:
            f()

    def at(fs, at_):
        return [(at_[min(i, len(at_) - 1)], f) for i, f in enumerate(fs)]

    ps = [T["ps%d" % i] for i in range(8)]
    XB = (4, 6)
    H = lambda h: slice(128 * h, 128 * h + 128)
    L8 = lambda h: slice(8 * h, 8 * h + 8)
    BMP, BMQ = [[-16, 8], [0, 16]], [[16, 8], [0, 16]]

    ms(T.one[:], 1.0, ["one"])
    ms(T.acn[:], 0, ["acn"])
    for n in ("em", "qm", "gm"):
        ms(T[n][:], 0.0, [n])
    dma("Y", [(T.n0s[:], T.n0[:])], (), ["n0s"])
    dma("Y", [(T.acs[:], T.acts[:])], (), ["acs"])
    dma("S", [(T.drp[:], T.dr[:])], (), ["drp"])
    dma("S", [(T.rg[:, 0:2048], T.regs[:])], (), ["rg"])
    dma("Y", [(T.rc[:], T.rch[:])], (), ["rc"])
    dma("Y", [(T.acn[16 * q:16 * q + 15, :], T.acts[16 * q + 1:16 * q + 16, :]) for q in range(8)], (), ["acn"])
    dma("Y", [(T.pys[:], T.pay[:])], (), ["pys"])

    iota(T.pmi[:], [[0, 16]], 0, 1, ["pmi"], False)
    sel(T.bm[:], T.one[:], BMP, OP.is_ge, 0.0, 0, 1, ["one"], ["bm"])
    sel(T.bm[:], T.bm[:], BMQ, OP.is_ge, 0.0, 15, -1, ["bm"], ["bm"])
    iota(T.jj[:], [[0, 16], [1, 16]], 0, 0, ["jj"], False)
    sel(T.idn[:], T.one[:], [[-1, 128]], OP.is_equal, 0.0, 0, 1, ["one"], ["idn"])
    ts(T.pma[:], T.pmi[:], 15, None, OP.bitwise_and, None, ["pmi"], ["pma"])
    cp(T.pc[:, 0:1], T.pma[:, 0:1], ["pma"], ["pc0"])
    ts(T.pc[:, 4:5], T.pc[:, 0:1], 1.0, 2.0 ** -17, OP.add, OP.mult, ["pc0"], ["pc4"])
    ts(T.lk[:, 0:128], T.bm[:], 64.0, None, OP.mult, None, ["bm"], ["lk"])
    ts(T.yx[:], T.jj[:], T.pc[:, 0:1], None, OP.subtract, None, ["jj", "pc0"], ["d256"])
    ts(T.dg[:], T.yx[:, 0:16], 0.0, None, OP.is_equal, None, ["d256"], ["dg"])
    ts(T.pc[:, 1:2], T.pc[:, 0:1], 15.0, BIG, OP.is_lt, OP.mult, ["pc0"], ["pc1"])
    ts(T.dr15[:], T.drp[:], 15, None, OP.bitwise_and, None, ["drp"], ["dr15"])
    cp(T.drb[:], T.drp[:], ["drp"], ["drb"])
    cp(T.drc[:], T.dr15[:], ["dr15"], ["drc"])

    def draw_rows(t):
        for j in range(8 * t, 8 * t + 8):
            if t:
                sel(T.ri[:, 128 * j:128 * j + 128], T.one[:], BMP, OP.is_equal, 0.0, -j, 1, ["one"], [("ri", j)])
            else:
                ts(T.ri[:, 128 * j:128 * j + 128], T.bm[:], T.dg[:, j:j + 1], None, OP.mult, None, ["bm", "dg"], [("ri", j)])

    def draws_a(t, ka, kb):
        for i in range(8):
            j, k, c = 8 * t + i, (ka, kb)[i // 4], 128 * (i % 4)
            mm(ps[k][:, c:c + 128], T.ri[:, 128 * j:128 * j + 128], T.drc[:], True, True, [("ri", j), "drc"], [("vp", k)], [k])
        ts(T.pk[:, 256 * t:256 * t + 256], ps[kb][:, 256:512], T.pc[:, 0:1], 16.0, OP.is_le, OP.mult, [("vp", kb), "pc0"], [("pkb", t)], [kb])
        for k, a, w in ((ka, 768 * t, 512), (kb, 768 * t + 512, 256)):
            act(T.uu[:, a:a + w], ps[k][:, 0:w], AF.Relu, [("vp", k), "pc4"], [("uu", t, k == kb)], [k], bias=T.pc[:, 4:5], scale=-2.0 ** -17)

    def draws_b(t, ka, kb):
        for i in range(8):
            j, k, c = 8 * t + i, (ka, kb)[i // 4], 128 * (i % 4)
            mm(ps[k][:, c:c + 128], T.ri[:, 128 * j:128 * j + 128], T.drb[:], True, True, [("ri", j), "drb"], [("vp", k)], [k])
        for k, a, w in ((ka, 768 * t, 512), (kb, 768 * t + 512, 256)):
            act(T.vv[:, a:a + w], ps[k][:, 0:w], AF.Identity, [("vp", k)], [("vv", t, k == kb)], [k], bias=2.0 ** -18, scale=1.0 / 64)
        act(ps[5][:, 0:256], ps[kb][:, 256:512], AF.Identity, [("vp", kb)], [("W", 0), ("W", 1)], [kb, 5], bias=1.0, scale=32.0)

    def draws_c(t):
        p = T.pk[:, 256 * t:256 * t + 256]
        tt(p, ps[5][:, 0:256], p, OP.add, [("W", 0), ("W", 1), ("pkb", t)], [("pk", t)], [5])

    def codes(lo, hi):
        for j in range(lo, hi):
            w = 1 << j
            act(T.cod[:, w:2 * w], T.cod[:, 0:w], AF.Identity, ["cod", "cb"], ["cod"], bias=T.cb[:, j:j + 1])

    draw_rows(0)
    act(T.bf1[:], T.bm[:], AF.Copy, ["bm"], ["bf1"])
    ts(T.cb[:], T.dg[:], 32.0, None, OP.mult, None, ["dg"], ["cb"])
    ts(T.ta[:, 0:1], T.pc[:, 0:1], 10.5, -16.0, OP.is_lt, OP.mult, ["pc0"], ["ta"])
    tt(T.cod[:, 0:1], T.ta[:, 0:1], T.dg[:, 11:12], OP.add, ["ta", "dg"], ["cod"])
    draws_a(0, 2, 3)
    draws_b(0, 0, 1)
    codes(0, 8)
    ts(T.thr[:], T.yx[:], 0.0, -4.0 * BIG, OP.is_le, OP.mult, ["d256"], ["dda"])
    ts(T.mq[:], T.yx[:], 1.0, BIG, OP.is_equal, OP.mult, ["d256"], ["ddb"])
    tt(T.dd[:], T.thr[:], T.mq[:], OP.add, ["dda", "ddb"], ["dd"])
    for w in (128, 256, 512, 1024):
        cp(T.lk[:, w:2 * w], T.lk[:, 0:w], ["lk"], ["lk"])
    for k in range(15):
        ms(T.lk[:, 128 * (k + 1) + k:2048:16], 0.0, [("lkz", k)] if k else ["lk"])
    LK = ["lk"] + [("lkz", k) for k in range(1, 15)]
    cp(T.n0u[:], T.n0s[:], ["n0s"], ["n0u"])
    for h in range(2):
        cp(T.a1[:, H(h)], T.acs[:].indirect(T.n0u[:, L8(h)]), ["acs", "n0u"], [("a1", h)])
    ts(T.xm0[:], T.rc[:], 1.0, None, OP.subtract, None, ["rc"], [("xm0", 0), ("xm0", 1)])

    def early(i):
        if i < 2:
            o = slice(512 * i, 512 * i + 512)
            tt(T.da[:, o], T.acs[:, o], T.acn[:, o], OP.subtract, ["acs", "acn"], [("da", i)])
        if i == 1:
            ts(T.nb0[:], T.n0s[:], 13.0, 1.0, OP.mult, OP.add, ["n0s"], [("nb0", 0), ("nb0", 1)])
            draws_c(0)
        if i == 2:
            act(T.bf5[:], T.bm[:], AF.Copy, ["bm"], ["bf5"], scale=5.0)
            ts(T.pc[:, 2:3], T.pc[:, 1:2], 1.0, None, OP.add, None, ["pc1"], ["pc2"])
            ts(T.pc[:, 3:4], T.pc[:, 1:2], -1.0 / 4096, None, OP.mult, None, ["pc1"], ["pc3"])
            for t in range(2):
                ms(T["zl%d" % t][:, 256:272], 0.0, [("zlz", t)])
            ts(T.t5[:], T.pmi[:], 4, 1, OP.logical_shift_right, OP.bitwise_and, ["pmi"], ["t5x", ("t5", 0), ("t5", 1)])
            cp(T.pc[:, 6:7], T.t5[:, 0:1], ["t5x"], ["pc6"])
            ts(T.pc[:, 5:6], T.pc[:, 6:7], -1.0, 1.0, OP.mult, OP.add, ["pc6"], ["pc5"])
            ts(T.b15[:], T.bm[:], T.dg[:, 15:16], None, OP.mult, None, ["bm", "dg"], ["b15"])

    iota(T.n13[:], [[13, 1024]], 3, 0, ["n13"])
    iota(T.posf0[:], [[-1, 256]], -1, 0, ["posf0"])
    iota(T.pri0[:], [[16, 16]], 0, 0, ["pri0"])
    iota(T.dmp[:], [[16, 16]], 2048, 0, ["dmp"])
    for j in range(8):
        iota(T.posf1[:, 32 * j:32 * j + 32], [[-1, 32]], -1 - 32 * order[j], 0, [("posf1", j)])
        iota(T.pri1[:, 2 * j:2 * j + 2], [[16, 2]], 32 * order[j], 0, [("pri1", j)])
    iota(T.onf[:], [[0, 128]], 1, 0, ["onf"])
    for t in range(2):
        iota(T["win%d" % t][:, 0:256], [[0, 256]], 0, 0, [("win", t)])
    iota(T.rg[:, 2048:2304], [[0, 256]], 0, 0, ["rgd"])
    D = [[-16, 8], [-1, 16]]
    for base, f in ((0, 1.0), (-8, 1.0), (1, -1.0), (-7, -1.0)):
        sel(T.em[:], T.em[:], D, OP.not_equal, f, base, 1, ["em"], ["em"])
    sel(T.em[:], T.em[:], [[0, 8], [-1, 16]], OP.is_ge, 0.0, 7, 0, ["em"], ["em"])
    sel(T.em[:], T.em[:], BMP, OP.is_ge, 0.0, 0, 1, ["em"], ["em"])
    sel(T.em[:], T.em[:], BMQ, OP.is_ge, 0.0, 15, -1, ["em"], ["em"])
    for k in range(16):
        sel(T.qm[:], T.qm[:], BMP, OP.not_equal, 32.0 * (pos[k % 8] - (pos[(k + 1) % 8] if k < 15 else 0)), -k, 1, ["qm"], ["qm"])
    for k in range(8):
        sel(T.gm[:], T.gm[:], BMP, OP.not_equal, 256.0 * (1 + pos[k]), -k, 1, ["gm"], ["gm"])
    draw_rows(1)

    def late():
        ts(T.dz[:], T.idn[:], 16.0, None, OP.mult, None, ["idn"], ["dz"])
        tt(T.dz[:], T.dz[:], T.bm[:], OP.subtract, ["dz", "bm"], ["dz"])
        ms(T.cod[:, 2048:2064], 0.0, ["codz"])
        cp(T.cod[:, 2048:2049], T.dg[:, 11:12], ["dg", "codz"], ["codz"])
        for n in range(2):
            pf = [("posf1", j) for j in range(8)] if n else ["posf0"]
            pr = [("pri1", j) for j in range(8)] if n else ["pri0"]
            act(T["pos%d" % n][:], T["posf%d" % n][:], AF.Copy, pf + ["dg"], ["pos%d" % n], scale=T.dg[:, 11:12])
            ts(T["ntr%d" % n][:], T["pri%d" % n][:], T.pc[:, 0:1], -2816.0, OP.add, OP.add, pr + ["pc0"], ["ntr%d" % n])
            ms(T["dv%d" % n][:], -8192.0, [("dv", n)])
            ms(T["da%d" % n][:], 0.0, [("dac", n)])
        ts(T.dmp[:], T.dmp[:], T.pc[:, 0:1], None, OP.add, None, ["dmp", "pc0"], ["dmp"])

    def reach(h, src, key):
        k = XB[h]
        mm(ps[k][:, 0:128], T.idn[:], src[:, H(h)], True, False, ["idn", key], [("xp", h)], [k])
        mm(ps[k][:, 0:128], T.idn[:], T.one[:], False, True, ["idn", "one"], [("xp", h)], [k])

    def records(h, A, key, part=False):
        for s in range(2):
            c = 2048 * h + 1024 * s
            w = T.rg[:, 0:2048]
            if part and s == 0:
                act(T.r[:, c:c + 512], w.indirect(A[:, 0:32]), AF.Relu, ["rg", key], [("r", h, s)])
                ts(T.r[:, c + 512:c + 1024], w.indirect(A[:, 32:64]), 0.0, None, OP.max, None, ["rg", key], [("r2", h, s)])
            else:
                act(T.r[:, c:c + 1024], w.indirect(A[:, 128 * h + 64 * s:128 * h + 64 * s + 64]), AF.Relu, ["rg", key], [("r", h, s), ("r2", h, s)])

    def mins(h, s, u, uo, ukey):
        c = 2048 * h + 1024 * s
        o = slice(64 * s, 64 * s + 64)
        x = ps[XB[h]][:, o]

        def one(k):
            if k == 0:
                mm(ps[h][:, o], T.idn[:], u[:, uo + 64 * s:uo + 64 * s + 64], True, False, ["idn", ukey], [("C", h)], [h])
            m = T.mn[:, c + 64 * k:c + 64 * k + 64]
            tt(m, T.r[:, c + k:c + 1024:16], x, OP.min, [("r", h, s), ("r2", h, s), ("xp", h)], [("mn", h, s, k)], [XB[h]])
            mm(ps[h][:, o], T.lk[:, 128 * k:128 * k + 128], m, False, k == 15, LK + [("mn", h, s, k)], [("C", h)], [h])
            mm(ps[2 + h][:, o], T.lk[:, 0:128], m, k == 0, k == 15, LK + [("mn", h, s, k)], [("M", h)], [2 + h])
        return [lambda k=k: one(k) for k in range(16)]

    def choose(h, v, vo, vkey, nu, nukey):
        def mask():
            tt(T.mk[:, H(h)], T.da[:].indirect(nu[:, L8(h)]), T.b[:, H(h)], OP.mult, [("da", 0), ("da", 1), nukey, ("b", h)], [("mk", h)])
            mm(ps[5][:, H(h)], T.bf1[:], T.mk[:, H(h)], True, True, ["bf1", ("mk", h)], [("W", h)], [5])
        return [lambda: tt(T.thr[:, H(h)], ps[2 + h][:, 0:128], v[:, vo:vo + 128], OP.mult, [("M", h), vkey], [("thr", h)], [2 + h]),
                lambda: tt(T.b[:, H(h)], ps[h][:, 0:128], T.thr[:, H(h)], OP.is_gt, [("C", h), ("thr", h)], [("b", h)], [h]),
                mask]

    def diag(out, okey, src, skey, h, bk):
        op("V", lambda e: e.tensor_tensor_scan(out[:, H(h)], T.dd[:, 0:128], src, 0.0, OP.add, OP.max), ["dd", skey], [okey], bk)

    def last(buf, h):
        return buf[:, 128 * h + 15:128 * h + 128:16]

    def rec_scan(h):
        diag(T.sc, ("sc", h), ps[5][:, H(h)], ("W", h), h, [5])

    def next_node(h, nb, nbkey):
        o = L8(h)
        return [lambda: ts(T.t5[:, o], last(T.sc, h), T.pc[:, 1:2], 5.0, OP.subtract, OP.mult, [("sc", h), "pc1"], [("t5", h)]),
                lambda: tt(T.t6[:, o], T.t5[:, o], nb[:, o], OP.add, [("t5", h), nbkey], [("t6", h)]),
                lambda: ts(T.ni[:, o], T.t6[:, o], 1023, None, OP.bitwise_and, None, [("t6", h)], [("ni", h)]),
                lambda: cp(T.nu[:, o], T.ni[:, o], [("ni", h)], [("nu", h)])]

    def names(h):
        cp(T.av[:, H(h)], T.acs[:].indirect(T.nu[:, L8(h)]), ["acs", ("nu", h)], [("av", h)])

    def rec_list(h):
        ts(T.ru[:, L8(h)], last(T.sc, h), T.pc[:, 1:2], None, OP.subtract, None, [("sc", h), "pc1"], [("ru", h)])

    def cut(h, src, skey, dst_, dkey):
        tt(dst_[:, H(h)], T.pt[:].indirect(T.ru[:, L8(h)]), src[:, H(h)], OP.min, ["pt", ("ru", h), skey], [dkey])

    ranges = [[[(0, 16 * c + 16)] for c in range(16)], []]
    for c in range(16):
        q = order[c // 2]
        a, b2 = sum(1 for p in same if p <= q), sum(1 for p in other if p <= q)
        ranges[1].append([(o, o + 32 * n) for o, n in ((0, a), (128, b2)) if n])
    plans = []
    for n in range(2):
        size = [sum(b - a for a, b in ranges[n][c]) for c in range(16)]
        by = sorted(range(16), key=lambda c: size[c])
        st = []
        for k, top in ((7, 512), (6, 300)):
            used = 0
            while used + size[by[0]] <= top:
                st.append((by[0], k, used))
                used += size[by.pop(0)]
        vt, room = [], [512] * 4
        for c in reversed(by):
            k = [k for k in range(4) if room[k] >= size[c]][0]
            vt.append((c, k, 512 - room[k]))
            room[k] -= size[c]
        vt.sort(key=lambda x: (x[1], x[2]))
        plans.append((size, st, vt))

    def firsts(n, t):
        o = slice(16 * n, 16 * n + 16)
        rk = [("recf", n, 0), ("recf", n, 1)]
        ts(T.ta[:], T.ded[:, o], 2048.0, None, OP.mult, None, [("ded", n, 0), ("ded", n, 1)], ["ta"])
        tt(T.rw[:], T.recf[:, o], T.ta[:], OP.max, rk + ["ta"], ["rw"])
        cp(T.rwu[:], T.rw[:], ["rw"], ["rwu"])
        for j in range(2):
            ts(T.tin[:, 16 * j:16 * j + 16], T.rw[:], T.pc[:, 5 + j:6 + j], None, OP.mult, None, ["rw", "pc5", "pc6"], [("tin", j)])
        op("V", lambda e: e.transpose(T.tou[:], T.tin[:]), [("tin", 0), ("tin", 1)], ["tou"])
        tt(T.tb[:], T.tou[:, 0:16], T.tou[:, 16:32], OP.add, ["tou"], ["tb"])
        cp(T.rwt[:], T.tb[:], ["tb"], ["rwt"])
        act(T.cl[:], T.cod[:].indirect(T.rwt[:]), AF.Copy, ["cod", "codz", "rwt"], ["cl"])
        tt(T.cr[:], T.cod[:].indirect(T.rwu[:]), T["pos%d" % n][:], OP.add, ["cod", "codz", "rwu", "pos%d" % n], ["cr"])
        for q in range(8):
            w = T.bdx[:, 256 * q:256 * q + 256]
            if q < 6:
                ts(w, T.cl[:], T.bf1[:, 16 * q:16 * q + 1], None, OP.mult, None, ["cl", "bf1"], [("bd", q)])
            else:
                act(w, T.cl[:], AF.Copy, ["cl", "bf1"], [("bd", q)], scale=T.bf1[:, 16 * q:16 * q + 1])
        size, st, vt = plans[n]
        bdk = [("bd", q) for q in range(8)]
        if n == 0 and t == 0:
            draws_a(1, 4, 6)
        for c, k, a in [x for x in vt if x[1] == 0] + st + [x for x in vt if x[1] != 0]:
            for lo, hi in ranges[n][c]:
                mm(ps[k][:, a:a + hi - lo], T.bdx[:, c:2048:16], T.cr[:, lo:hi], True, True, bdk + ["cr"], [("dt", k)], [k])
                a += hi - lo
        for c, k, a in st:
            j = 512 * (k == 6) + a
            act(T.jk[:, j:j + size[c]], ps[k][:, a:a + size[c]], AF.Relu, [("dt", k), "ntr%d" % n, ("dac", n)], [("jk", n, c), ("dacx", n, c)], [k],
                bias=T["ntr%d" % n][:, c:c + 1], accum_out=T["da%d" % n][:, c:c + 1])
        for c in range(16):
            lastw[("jk", 1 - n, c)] = lastw[("jk", n, st[-1][0])]

    def most(n):
        size, st, vt = plans[n]
        for c, k, a in vt:
            op("V", lambda e: e.tensor_reduce(T["dv%d" % n][:, c:c + 1], ps[k][:, a:a + size[c]], AxisListType.X, OP.max),
               [("dt", k), ("dv", n)], [("dvx", n, c)], [k])

    def firsts2(n):
        o = slice(16 * n, 16 * n + 16)
        rk = [("recf", n, 0), ("recf", n, 1)]
        size, st, vt = plans[n]
        dvk = [("dv", n)] + [("dvx", n, c) for c, _, _ in vt]
        return [
            lambda: tt(T.ta[:], T["dv%d" % n][:], T["ntr%d" % n][:], OP.add, dvk + ["ntr%d" % n], ["ta"]),
            lambda: tt(T.tb[:], T.ta[:], T["da%d" % n][:], OP.max, ["ta", ("dac", n)] + [("dacx", n, c) for c, _, _ in st], ["tb"]),
            lambda: ts(T.ta[:], T.tb[:], 0.0, None, OP.is_gt, None, ["tb"], ["ta"]),
            lambda: tt(T.tb[:], T.ta[:], T.ded[:, o], OP.max, ["ta", ("ded", n, 0), ("ded", n, 1)], ["tb"]),
            lambda: tt(T.ta[:], T.tb[:], T.dmp[:], OP.mult, ["tb", "dmp"], ["ta"]),
            lambda: tt(T.of[:], T.ta[:], T.recf[:, o], OP.max, ["ta"] + rk, ["of"]),
            lambda: cp(T.ofu[:, o], T.of[:], ["of"], [("ofu", n)])]

    def change(n, z, zk, sign):
        w = T.rg[:].indirect(T.ofu[:, 16 * n:16 * n + 16])
        tt(T.ch[:], w, z, sign, ["rg", "rgd", ("ofu", n)] + zk, ["ch"])
        ts(T.ci[:], T.ch[:], 15.0, -15.0, OP.min, OP.max, ["ch"], ["ci"])
        cp(w, T.ci[:], ["ci", ("ofu", n)], ["rg", "rgd"])

    mates = [q for q in same if q != me]
    off = topo.engines(core, T.cores[mates[0]])
    onc = split(topo.engines(core, rel[0]), 2)

    def send_relay(buf, key, rbuf, sem):
        trs = [RemoteDMATransfer(dst_ids=[dst(rel[j], core, topo)], dma_engine_mask=bits(onc[j]), remote_sem=T.sem[sem],
                                 src=buf[:, 128 + 64 * j:192 + 64 * j], dst=T[rbuf][:, 0:64]) for j in range(2)]
        nloc[0] += sum(len(x) for x in onc)
        remote(trs, key)

    def send_same(buf, key, land, sem):
        trs = []
        for es, q in zip(share(off, len(mates)), mates):
            d = T.cores[q]
            p = places(d, T, topo)[0].index(me)
            trs.append(RemoteDMATransfer(dst_ids=[dst(d, core, topo)], dma_engine_mask=bits(es), remote_sem=T.sem[sem],
                                         src=buf[:, 32 * pos[q]:32 * pos[q] + 32], dst=T[land][:, 32 * p:32 * p + 32]))
            nloc[0] += len(es)
        remote(trs, key)

    na = nb_ = 0
    for q in mates:
        d = T.cores[q]
        m2 = [x for x in places(d, T, topo)[0] if x != q]
        na += len(share(topo.engines(d, core), len(m2))[m2.index(me)])
    for q in other:
        i = places(T.cores[q], T, topo)[1].index(me)
        nb_ += len(split(topo.engines(relays(T.cores[q], T, topo)[i // 2], core), 2)[i % 2])

    own = 32 * pos[me]
    CP, SP, WP, KP = (0, 2, 4), (8, 9, 11, 12, 14, 15, 16, 21, 23, 25, 27), (6, 8, 10, 12), range(15, 25)
    for t in range(2):
        win, land, zb, zl = T["win%d" % t], T["land%d" % t], T["zb%d" % t], T["zl%d" % t]

        def lev(e, h):
            o = 256 * (e - 1) + 128 * h
            return dict(uo=768 * t + o, uk=("uu", t, o >= 512), vk=("vv", t, o >= 512), nu=T.n0u if e == 1 else T.nu,
                        nk="n0u" if e == 1 else ("nu", h), nb=T.nb0 if e == 1 else T.nb, bk=("nb0", h) if e == 1 else ("nb", h),
                        x=(T.xm0, T.xm, T.xn)[e - 1], xk=(("xm0", "xm", "xn")[e - 1], h),
                        x2=(T.xm, T.xn, T.xm)[e - 1], x2k=(("xm", "xn", "xm")[e - 1], h))

        def m_(e, h):
            d = lev(e, h)
            return mins(h, 0, T.uu, d["uo"], d["uk"]) + mins(h, 1, T.uu, d["uo"], d["uk"])

        def c_(e, h):
            d = lev(e, h)
            return choose(h, T.vv, d["uo"], d["vk"], d["nu"], d["nk"])

        def step(e, h):
            d = lev(e, h)
            nn = next_node(h, d["nb"], d["bk"])

            def go():
                names(h)
                records(h, T.av, ("av", h))
            r = [lambda: rec_scan(h), nn[0], lambda: rec_list(h)] + nn[1:] + [go, lambda: cut(h, d["x"], d["xk"], d["x2"], d["x2k"]),
                 lambda: reach(h, d["x2"], d["x2k"])]
            if e == 1:
                r.append(lambda: ts(T.nb[:, L8(h)], T.ni[:, L8(h)], 13.0, 2.0, OP.mult, OP.add, [("ni", h)], [("nb", h)]))
            if t == 0 and h:
                r.append(lambda: codes(*((8, 10) if e == 1 else (10, 11))))
            return r

        def way(h):
            E, o, k = ps[7][:, 256 * h + 128:256 * h + 256], slice(256 * h, 256 * h + 128), XB[h]
            ini = T.cum[:, 127:128] if h else 0.0

            def a():
                mm(E, T.em[:], T.b[:, H(h)], True, True, ["em", ("b", h)], [("E", h)], [7])
                if h:
                    act(T.mq[:, H(h)], T.n13[:].indirect(T.nu[:, L8(h)]), AF.Copy, ["n13", ("nu", h)], [("mq", h)])
                else:
                    cp(T.mq[:, H(h)], T.n13[:].indirect(T.nu[:, L8(h)]), ["n13", ("nu", h)], [("mq", h)])

            def b():
                op("V", lambda e: e.tensor_tensor_scan(T.cum[:, H(h)], T.onf[:], E, ini, OP.mult, OP.add),
                   ["onf", ("E", h)] + ([("cum", 0)] if h else []), [("cum", h)], [7])

            def d():
                ts(T.gg[:, H(h)], T.ff[:, H(h)], 32.0, None, OP.is_gt, None, [("ff", h)], [("gg", h)])
                mm(ps[7][:, o], T.qm[:], T.b[:, H(h)], True, False, ["qm", ("b", h)], [("sl", h)], [7])
                mm(ps[7][:, o], T.bm[:], T.ff[:, H(h)], False, False, ["bm", ("ff", h)], [("sl", h)], [7])
                mm(ps[7][:, o], T.gm[:], T.gg[:, H(h)], False, True, ["gm", ("gg", h)], [("sl", h)], [7])
                mm(ps[k][:, 128:256], T.bf5[:], T.mk[:, H(h)], True, False, ["bf5", ("mk", h)], [("T", h)], [k])
                mm(ps[k][:, 128:256], T.b15[:], T.mq[:, H(h)], False, True, ["b15", ("mq", h)], [("T", h)], [k])
            return [a, b, lambda: tt(T.ff[:, H(h)], E, T.cum[:, H(h)], OP.mult, [("E", h), ("cum", h)], [("ff", h)], [7]), d]

        def pack(h):
            p, k = ps[5][:, 256 + 128 * h:384 + 128 * h], XB[h]
            return [
                lambda: rec_scan(h),
                lambda: rec_list(h),
                lambda: diag(T.ss, ("ssn", h), ps[7][:, 256 * h:256 * h + 128], ("sl", h), h, [7]),
                lambda: cut(h, T.xn, ("xn", h), T.xm, ("xm", h)),
                lambda: ts(T.su[:, L8(h)], last(T.ss, h), T.pc[:, 2:3], None, OP.subtract, None, [("ssn", h), "pc2"], [("su", h)]),
                lambda: ts(T.ti[:, H(h)], ps[k][:, 128:256], 4096.0, None, OP.mult, None, [("T", h)], [("ti", h)], [k]),
                lambda: tt(p, T.xm[:, H(h)], T.pk[:, 256 * t + 128 * h:256 * t + 128 * h + 128], OP.add, [("xm", h), ("pk", t)], [("yx", h)], [5]),
                lambda: ts(T.tj[:, H(h)], T.ti[:, H(h)], 1023 * 4096, None, OP.bitwise_and, None, [("ti", h)], [("tj", h)]),
                lambda: tt(T.y[:, H(h)], T.tj[:, H(h)], p, OP.add, [("tj", h), ("yx", h)], [("y", h)], [5]),
                lambda: cp(win[:].indirect(T.su[:, L8(h)]), T.y[:, H(h)], [("su", h), ("y", h)], [("win", t)])]

        def lists(h):
            ts(T.recf[:, L8(h)], last(T.sc, h), T.pc[:, 1:2], None, OP.subtract, None, [("sc", h), "pc1"], [("recf", 0, h)])
            ts(T.ded[:, L8(h)], last(T.ss, h), T.pc[:, 2:3], 255.5, OP.subtract, OP.is_gt, [("ssn", h), "pc2"], [("ded", 0, h)])
            ts(T.zo[:, L8(h)], last(T.ss, h), T.pc[:, 2:3], 256.0, OP.subtract, OP.min, [("ssn", h), "pc2"], [("zo", h)])

        for h in range(2):
            records(h, T.a1, ("a1", h), h == 0)
            reach(h, T.xm0, ("xm0", h))
        if t == 0:
            early(0)
        r = m_(1, 0)
        if t == 0:
            r.insert(16, lambda: early(1))
        r.insert(17, lambda: ts(T.pt[:], T.rg[:, 0:2048], 0.0, None, OP.max, None, ["rg"], ["pt"]))
        for f in r:
            f()
        for e in (1, 2):
            x = at([lambda: early(2)], (14,)) if e == 1 and t == 0 else []
            weave(m_(e, 1), at(c_(e, 0), CP) + x + at(step(e, 0), SP))
            weave(m_(e + 1, 0), at(c_(e, 1), CP) + at(step(e, 1), SP))
        weave(m_(3, 1), at(c_(3, 0), CP) + at(way(0), WP) + at(pack(0), KP))
        lists(0)
        for f in c_(3, 1) + way(1) + pack(1):
            f()
        send_relay(win, [("win", t)], "rl%d" % t, "rq%d" % t)
        send_same(win, [("win", t)], "land%d" % t, "ha%d" % t)
        act(land[:, own:own + 32], win[:, own:own + 32], AF.Copy, [("win", t)], [("lown", t)])
        ext(("lnd", t, 0), "ha%d" % t, na)
        ext(("lnd", t, 1), "hb%d" % t, nb_)
        lists(1)
        if t == 0:
            late()
        firsts(0, t)

        def far_in(h):
            lk = [("lnd", t, h)] + ([] if h else [("lown", t)])
            op("V", lambda e: e.tensor_tensor_scan(T.ss[:, H(h)], T.dd[:, 0:128], land[:, H(h)], 0.0, OP.add, OP.max), ["dd"] + lk, [("ssn", h)])
            ts(T.nu[:, L8(h)], last(T.ss, h), 1.0 / 4096, T.pc[:, 3:4], OP.mult, OP.add, [("ssn", h), "pc3"], [("nu", h)])
            names(h)
            records(h, T.av, ("av", h))
            cp(T.yi[:, H(h)], land[:, H(h)], lk, [("yi", h)])
            ts(T.yj[:, H(h)], T.yi[:, H(h)], 15, None, OP.bitwise_and, None, [("yi", h)], [("yj", h)])
            cp(ps[XB[h]][:, 0:128], T.yj[:, H(h)], [("yj", h)], [("xp", h)], [XB[h]])
            ts(T.yk[:, H(h)], T.yi[:, H(h)], 4, 1, OP.logical_shift_right, OP.bitwise_and, [("yi", h)], [("yk", h)])
            ts(T.u4[:, H(h)], T.yk[:, H(h)], 2.0 ** -13, None, OP.mult, None, [("yk", h)], [("u4", h)])

        def far_in2(h):
            a = L8(h)
            return [
                lambda: ts(T.yo[:, H(h)], T.yi[:, H(h)], 5, 63, OP.logical_shift_right, OP.bitwise_and, [("yi", h)], [("yo", h)]),
                lambda: ts(T.v4[:, H(h)], T.yo[:, H(h)], 1.0 / 64, 2.0 ** -18, OP.mult, OP.add, [("yo", h)], [("v4", h)]),
                lambda: ts(T.xm[:, H(h)], T.yj[:, H(h)], 1.0, None, OP.subtract, None, [("yj", h)], [("xm", h)]),
                lambda: cp(T.ni[:, a], T.nu[:, a], [("nu", h)], [("ni", h)]),
                lambda: ts(T.nb[:, a], T.ni[:, a], 13.0, 4.0, OP.mult, OP.add, [("ni", h)], [("nb", h)]),
                lambda: ts(T.yl[:, a], last(T.ss, h), T.pc[:, 1:2], None, OP.subtract, None, [("ssn", h), "pc1"], [("yl", h)]),
                lambda: ts(T.ym[:, a], T.yl[:, a], 15, None, OP.bitwise_and, None, [("yl", h)], [("ym", h)]),
                lambda: ts(T.ded[:, 16 + 8 * h:24 + 8 * h], T.ym[:, a], 1.0, None, OP.is_lt, None, [("ym", h)], [("ded", 1, h)])]

        def leaf(h):
            E = ps[7][:, 256 * h + 128:256 * h + 256]
            nn = next_node(h, T.nb, ("nb", h))

            def sign():
                tt(T.val[:, H(h)], T.pys[:].indirect(T.nu[:, L8(h)]), T.xr[:, H(h)], OP.min, ["pys", ("nu", h), ("xr", h)], [("val", h)])
                mm(E, T.dz[:], T.val[:, H(h)], True, True, ["dz", ("val", h)], [("E", h)], [7])
                act(zb[:, H(h)], E, AF.Sign, [("E", h)], [("zb", t, h)], [7])
                if h:
                    send_relay(zb, [("zb", t, 1)], "rz%d" % t, "rv%d" % t)
                else:
                    send_same(zb, [("zb", t, 0)], "zl%d" % t, "za%d" % t)
                    act(zl[:, own:own + 32], zb[:, own:own + 32], AF.Copy, [("zb", t, 0)], [("zown", t)])

            return [lambda: rec_scan(h), nn[0], lambda: rec_list(h), nn[1], nn[2], lambda: cut(h, T.xm, ("xm", h), T.xn, ("xn", h)), nn[3],
                    lambda: ts(T.xr[:, H(h)], T.xn[:, H(h)], 1.0, None, OP.add, None, [("xn", h)], [("xr", h)]), sign,
                    lambda: ts(T.recf[:, 16 + 8 * h:24 + 8 * h], last(T.sc, h), T.pc[:, 1:2], None, OP.subtract, None, [("sc", h), "pc1"], [("recf", 1, h)])]

        far_in(0)
        most(0)
        m4 = [mins(h, 0, T.u4, 128 * h, ("u4", h)) + mins(h, 1, T.u4, 128 * h, ("u4", h)) for h in range(2)]
        c4 = [choose(h, T.v4, 128 * h, ("v4", h), T.nu, ("nu", h)) for h in range(2)]
        a, b = far_in2(0), firsts2(0)
        mix = [f for p in zip(a, b) for f in p] + a[len(b):]
        weave(m4[0], sorted(at(mix, (0, 0, 0, 2, 4, 6, 8, 10, 12, 14, 15)) + [(14, lambda: far_in(1))] + at(far_in2(1), range(18, 26)), key=lambda x: x[0]))
        weave(m4[1], at(c4[0], CP) + at(leaf(0), SP))
        for f in c4[1] + leaf(1):
            f()
        ext(("zrl", t, 0), "za%d" % t, na)
        ext(("zrl", t, 1), "zb%d" % t, nb_)
        firsts(1, t)
        most(1)
        for f in firsts2(1):
            f()
        if t == 0:
            draws_b(1, 4, 6)
            draws_c(1)
        change(1, zb[:], [("zb", t, 0), ("zb", t, 1)], OP.add)
        zk = [("zrl", t, 0), ("zrl", t, 1), ("zown", t), ("zlz", t)]
        cp(T.zg[:, 0:128], zl[:].indirect(T.zo[:, 0:8]), zk + [("zo", 0)], [("zg", 0)])
        act(T.zg[:, 128:256], zl[:].indirect(T.zo[:, 8:16]), AF.Copy, zk + [("zo", 1)], [("zg", 1)])
        change(0, T.zg[:], [("zg", 0), ("zg", 1)], OP.subtract)
    dma("Y", [(T.yr[:], T.rg[:, 0:2048])], ["rg"], ["yr"])
    total["loc"] = nloc[0]
    for s, v in total.items():
        g.wait_ge(T.sem[s], v)
